import numpy as np
import ml_dtypes


def mxq(x, axis, fmt="e4m3"):
    dtype, down = {"e4m3": (ml_dtypes.float8_e4m3fn, 7), "e5m2": (ml_dtypes.float8_e5m2, 14)}[fmt]
    v = np.moveaxis(np.asarray(x, np.float32).astype(ml_dtypes.bfloat16).astype(np.float64), axis, -1)
    blocks = v.reshape(v.shape[:-1] + (-1, 32))
    amax = np.abs(blocks).max(-1, keepdims=True)
    byte = np.maximum(np.where(amax > 0, np.frexp(amax)[1] - 1 + 127, 0) - down, 1)
    scale = np.exp2(byte - 127.0)
    codes = (blocks / scale).astype(np.float32).astype(dtype).astype(np.float64)
    return np.moveaxis((codes * scale).reshape(v.shape), -1, axis)


WIDE = False


def mx_kscale(k):
    if not WIDE:
        return np.ones(k)
    levels = np.array([10, -10, 5, -5, 0])
    if k % 512:
        return np.exp2(np.random.permutation(np.resize(levels, k // 32))).repeat(32)
    a = np.empty((k // 512, 16))
    for p in range(k // 512):
        a[p, :8] = np.random.permutation(np.resize(levels, 8))
        for g in range(8):
            far = levels[np.abs(levels - a[p, g]) >= 10]
            a[p, g + 8] = far[np.random.randint(len(far))]
    return np.exp2(a.ravel()).repeat(32)


def f64(x):
    return np.asarray(x).astype(np.float64)


def striped(idx):
    return np.tile(idx.reshape(-1, 16).T, (8, 1)).astype(np.uint16)


def unstriped(offs):
    return offs[:16].T.reshape(-1).astype(np.int64)


E2M1 = np.array([0.0, 0.5, 1.0, 1.5, 2.0, 3.0, 4.0, 6.0, -0.0, -0.5, -1.0, -1.5, -2.0, -3.0, -4.0, -6.0])


def pack_weight(w, fmt):
    k, n = w.shape
    w = f64(np.asarray(w, np.float32).astype(ml_dtypes.bfloat16)).reshape(k // 32, 32, n)
    amax = np.abs(w).max(1)
    if fmt == "e4m3":
        byte = np.frexp(amax)[1] - 1 + 127 - 7
    else:
        mant, ex = np.frexp(amax / 6.0)
        byte = np.where(mant > 0.5, ex, ex - 1) + 127
    byte = np.clip(np.where(amax > 0, byte, 1), 1, 254)
    scaled = (w * np.exp2(127.0 - byte)[:, None, :]).reshape(k, n).astype(np.float32)
    by_word = np.ascontiguousarray(scaled.reshape(k // 512, 128, 4, n).transpose(0, 1, 3, 2))
    if fmt == "e4m3":
        words = by_word.astype(ml_dtypes.float8_e4m3fn).view(np.uint8)
    else:
        c = by_word.astype(ml_dtypes.float4_e2m1fn).view(np.uint8) & 0xF
        words = (c[..., 0::2] | (c[..., 1::2] << 4)).reshape(k // 512, 128, 2 * n)
    return np.ascontiguousarray(words), np.ascontiguousarray(byte.astype(np.uint8).reshape(k // 512, 16, n))


def unpack_weight(words, scales, fmt):
    g, _, n = scales.shape
    words = np.ascontiguousarray(words).reshape(g, 128, n, -1)
    if fmt == "e4m3":
        vals = words.view(ml_dtypes.float8_e4m3fn).astype(np.float64)
    else:
        nib = np.empty((g, 128, n, 4), np.uint8)
        nib[..., 0::2] = words & 0xF
        nib[..., 1::2] = words >> 4
        vals = E2M1[nib]
    vals = vals * np.repeat(np.exp2(scales.astype(np.float64) - 127.0), 8, axis=1)[..., None]
    return vals.transpose(0, 1, 3, 2).reshape(g * 512, n)


def silu(v):
    return v / (1.0 + np.exp(-np.maximum(v, -700.0)))


def d_silu(v):
    s = 1.0 / (1.0 + np.exp(-np.maximum(v, -700.0)))
    return s * (1.0 + v * (1.0 - s))


K, T, E, C, H, N = 512, 512, 4, 128, 512, 1024


def by_expert(wq, xq):
    return np.concatenate([wq[e].T @ xq[:, e * C:(e + 1) * C] for e in range(E)], axis=1)


def setup_inputs():
    n = np.random.standard_normal
    s = mx_kscale(N)[:, None]
    u = mx_kscale(H)
    dy = pack_weight(n((N, T)) * s, "e4m3")
    w2 = [pack_weight(m, "e2m1") for m in n((E, N, H)) / np.sqrt(N) / s[None] * u[None, None, :]]
    w1 = [pack_weight(m, "e2m1") for m in n((E, H, K)) / np.sqrt(H) / u[None, :, None]]
    w3 = [pack_weight(m, "e2m1") for m in n((E, H, K)) / np.sqrt(H) / u[None, :, None]]
    return {
        "dy_words": dy[0],
        "dy_scales": dy[1],
        "a1": n((H, E * C)).astype(np.float32),
        "a3": n((H, E * C)).astype(np.float32),
        "w2_words": np.stack([m[0] for m in w2]),
        "w2_scales": np.stack([m[1] for m in w2]),
        "w1_words": np.stack([m[0] for m in w1]),
        "w1_scales": np.stack([m[1] for m in w1]),
        "w3_words": np.stack([m[0] for m in w3]),
        "w3_scales": np.stack([m[1] for m in w3]),
        "gate": np.tile(np.random.uniform(0.2, 1.0, E * C), (H, 1)).astype(np.float32),
        "offs": striped(np.random.permutation(T)[:E * C]),
    }


def reference(dy_words, dy_scales, a1, a3, w2_words, w2_scales, w1_words, w1_scales, w3_words, w3_scales, gate, offs):
    idx = unstriped(offs)
    w2 = np.stack([unpack_weight(w2_words[e], w2_scales[e], "e2m1") for e in range(E)])
    w1 = np.stack([unpack_weight(w1_words[e], w1_scales[e], "e2m1") for e in range(E)])
    w3 = np.stack([unpack_weight(w3_words[e], w3_scales[e], "e2m1") for e in range(E)])
    gq = unpack_weight(dy_words, dy_scales, "e4m3")[:, idx]
    dh = f64(gate) * by_expert(w2, gq)
    da1 = dh * f64(a3) * d_silu(f64(a1))
    da3 = dh * silu(f64(a1))
    dx = by_expert(w1, mxq(da1, 0, "e4m3")) + by_expert(w3, mxq(da3, 0, "e4m3"))
    out = np.zeros((K, T))
    out[:, idx] = dx
    return out

@@ -1,0 +1,174 @@
+from contextlib import ExitStack
+
+import concourse.mybir as mybir
+from concourse.masks import make_identity
+
+K, T, E, C, H, N = 512, 512, 4, 128, 512, 1024
+FLOPS = 2 * E * C * (N * H + 2 * H * K)
+
+F32 = mybir.dt.float32
+BF16 = mybir.dt.bfloat16
+I32 = mybir.dt.int32
+U32 = mybir.dt.uint32
+U16 = mybir.dt.uint16
+U8 = mybir.dt.uint8
+FP8X4 = mybir.dt.float8_e4m3fn_x4
+FP4X4 = mybir.dt.float4_e2m1fn_x4
+ACT = mybir.ActivationFunctionType
+ALU = mybir.AluOpType
+
+P = 128
+PASSES = N // 512
+KT = K // P
+LIST_COLS = C // 16
+
+
+def tile_moe_bdx_glu_silu_kernel(
+    tc, dy_words, dy_scales, a1, a3, w2_words, w2_scales, w1_words, w1_scales, w3_words, w3_scales, gate, offs, out
+):
+    nc = tc.nc
+    with ExitStack() as ctx:
+        keep = ctx.enter_context(tc.tile_pool(name="keep", bufs=1))
+        work = ctx.enter_context(tc.tile_pool(name="work", bufs=2))
+        ps_dh = ctx.enter_context(tc.psum_pool(name="ps_dh", bufs=2))
+        ps_tr = ctx.enter_context(tc.psum_pool(name="ps_tr", bufs=3))
+        ps_dx = ctx.enter_context(tc.psum_pool(name="ps_dx", bufs=2))
+
+        offsets = keep.tile([P, E * LIST_COLS], U16, name="offsets")
+        dy_w = keep.tile([P, PASSES, T], I32, name="dy_w", align_bytes=64)
+        dy_s = keep.tile([P, PASSES, T], U8, name="dy_s", align_bytes=64)
+        w2_s = keep.tile([P, E * PASSES, H], U8, name="w2_s", align_bytes=64)
+        w1_s = keep.tile([P, E, K], U8, name="w1_s", align_bytes=64)
+        w3_s = keep.tile([P, E, K], U8, name="w3_s", align_bytes=64)
+        ident = keep.tile([P, P], F32, name="ident", align_bytes=64)
+        gate_col = keep.tile([P, E], F32, name="gate_col")
+        warm = keep.tile([P, 2], F32, name="warm")
+
+        for plane in (dy_s, w2_s, w1_s, w3_s):
+            nc.vector.memset(plane[:].rearrange("p a b -> p (a b)").bitcast(I32), 0)
+        nc.gpsimd.memset(warm[:, 0:1], 0.0)
+        nc.scalar.activation(warm[:, 1:2], warm[:, 0:1], ACT.Silu)
+
+        def load_scales(queue, plane, rows):
+            by_row = rows.rearrange("a (q r) n -> r q a n", r=4)
+            for r in range(4):
+                queue.dma_start(out=plane[r:P:32, :, :].bitcast(I32), in_=by_row[r].bitcast(I32))
+
+        groups = [(0, 1), (1, 2), (2, 4)]
+        w2_w, w1_w, w3_w, a1_t, a3_t = {}, {}, {}, {}, {}
+
+        def load_words(name, table, src, lo, hi):
+            passes = src.shape[1]
+            t = keep.tile([P, (hi - lo) * passes, 1024], U8, name="%s_%d" % (name, lo), align_bytes=64)
+            nc.sync.dma_start(out=t[:].bitcast(I32), in_=src[lo:hi].rearrange("e s p b -> p (e s) b").bitcast(I32))
+            for e in range(lo, hi):
+                table[e] = t[:, (e - lo) * passes : (e - lo + 1) * passes, :]
+
+        def load_saved(name, table, src, lo, hi):
+            t = keep.tile([P, 4, (hi - lo) * C], F32, name="%s_%d" % (name, lo), align_bytes=64)
+            nc.sync.dma_start(out=t[:], in_=src.rearrange("(p t) j -> p t j", t=4)[:, :, lo * C : hi * C])
+            for e in range(lo, hi):
+                table[e] = t[:, :, (e - lo) * C : (e - lo + 1) * C]
+
+        nc.sync.dma_start(offsets[:], offs)
+        nc.sync.dma_start(out=dy_w[:], in_=dy_words.rearrange("o p t d -> p o (t d)").bitcast(I32))
+        load_scales(nc.sync, dy_s, dy_scales)
+        load_words("w2", w2_w, w2_words, 0, 1)
+        load_saved("a1", a1_t, a1, 0, 1)
+        load_scales(nc.gpsimd, w2_s, w2_scales.rearrange("e s f n -> (e s) f n"))
+        with nc.allow_non_contiguous_dma(reason="one gate value to a partition"):
+            nc.gpsimd.dma_start(out=gate_col[:], in_=gate[0].rearrange("(e c) -> c e", e=E))
+        make_identity(nc, ident[:])
+        load_saved("a3", a3_t, a3, 0, 1)
+        load_words("w2", w2_w, w2_words, 1, 2)
+        load_saved("a1", a1_t, a1, 1, 2)
+        load_words("w1", w1_w, w1_words, 0, 2)
+        load_words("w3", w3_w, w3_words, 0, 2)
+        load_saved("a3", a3_t, a3, 1, 2)
+        load_scales(nc.sync, w1_s, w1_scales.rearrange("e s f n -> (e s) f n"))
+        load_scales(nc.sync, w3_s, w3_scales.rearrange("e s f n -> (e s) f n"))
+        load_words("w2", w2_w, w2_words, 2, 4)
+        load_saved("a1", a1_t, a1, 2, 4)
+        load_saved("a3", a3_t, a3, 2, 4)
+        load_words("w1", w1_w, w1_words, 2, 4)
+        load_words("w3", w3_w, w3_words, 2, 4)
+
+        g_w, g_s = {}, {}
+        for lo, hi in ((0, 1), (1, 4)):
+            picks = offsets[:, lo * LIST_COLS : hi * LIST_COLS]
+            for s in range(PASSES):
+                words = keep.tile([P, (hi - lo) * C], U32, name="g_w_%d_%d" % (lo, s), align_bytes=64)
+                nc.vector.tensor_copy(words[:], dy_w[:, s, :].bitcast(U32).indirect(picks))
+                for e in range(lo, hi):
+                    g_w[e, s] = words[:, (e - lo) * C : (e - lo + 1) * C]
+            for s in range(PASSES):
+                scales = keep.tile([P, (hi - lo) * C], U8, name="g_s_%d_%d" % (lo, s), align_bytes=64)
+                nc.vector.tensor_copy(scales[:], dy_s[:, s, :].indirect(picks))
+                for e in range(lo, hi):
+                    g_s[e, s] = scales[:, (e - lo) * C : (e - lo + 1) * C]
+
+        windows = [keep.tile([P, T], F32, name="window_%d" % kt, align_bytes=64) for kt in range(KT)]
+        dx_sb = {}
+
+        def scatter(e):
+            picks = offsets[:, e * LIST_COLS : (e + 1) * LIST_COLS]
+            for kt in range(KT):
+                nc.vector.tensor_copy(windows[kt][:].indirect(picks), dx_sb[e][:, kt, :])
+                if e == E - 1:
+                    nc.sync.dma_start(out=out[kt * P : (kt + 1) * P, :], in_=windows[kt][:])
+
+        def by_fours(ap):
+            return ap.rearrange("p t (c i) -> p c t i", i=4)
+
+        for e in range(E):
+            silu_neg = work.tile([P, 4, C], F32, name="silu_neg")
+            nc.scalar.activation(silu_neg[:], a1_t[e], ACT.Silu, scale=-1.0)
+            half_rest = work.tile([P, 4, C], F32, name="half_rest")
+            nc.scalar.activation(half_rest[:], silu_neg[:], ACT.Copy, scale=-0.5, bias=0.5)
+            tanh_half = work.tile([P, 4, C], F32, name="tanh_half")
+            nc.scalar.activation(tanh_half[:], a1_t[e], ACT.Tanh, scale=0.5)
+
+            dh_ps = ps_dh.tile([P, H], F32, name="dh_ps")
+            for s in range(PASSES):
+                nc.tensor.matmul_mx(
+                    dh_ps[:], lhsT=g_w[e, s].bitcast(FP8X4), lhsT_scale=g_s[e, s],
+                    rhs=w2_w[e][:, s, :].bitcast(FP4X4), rhs_scale=w2_s[:, e * PASSES + s, :],
+                    start=(s == 0), stop=(s == PASSES - 1),
+                )
+            dh_sb = work.tile([P, 4, P], F32, name="dh_sb", align_bytes=64)
+            nc.scalar.activation(dh_sb[:], dh_ps[:].rearrange("c (p t) -> c t p", t=4), ACT.Copy, scale=gate_col[:, e : e + 1])
+            dh = ps_tr.tile([P, 4, C], F32, name="dh")
+            for t in range(4):
+                nc.tensor.transpose(dh[:, t, :], dh_sb[:, t, :], ident[:])
+            factor3 = work.tile([P, 4, C], F32, name="factor3")
+            nc.scalar.activation(factor3[:], a1_t[e], ACT.Silu)
+
+            part = work.tile([P, 4, C], F32, name="part")
+            nc.vector.tensor_tensor(part[:], half_rest[:], a3_t[e], ALU.mult)
+            factor1 = work.tile([P, 4, C], F32, name="factor1")
+            nc.vector.scalar_tensor_tensor(factor1[:], tanh_half[:], 1.0, part[:], ALU.add, ALU.mult)
+            da = work.tile([P, 2, C, 4], BF16, name="da", align_bytes=64)
+            for which, factor in ((1, factor3), (0, factor1)):
+                nc.vector.tensor_tensor(
+                    da[:, which].rearrange("p (c i) t -> p c t i", i=4), by_fours(dh[:]), by_fours(factor[:]), ALU.mult
+                )
+            codes = work.tile([P, 2 * C], U32, name="codes", align_bytes=64)
+            da_s = work.tile([P, 2 * C], U8, name="da_s", align_bytes=64)
+            nc.vector.quantize_mx(codes[:].bitcast(FP8X4), da_s[:], da[:].rearrange("p w j t -> p (w j t)"))
+
+            dx_ps = ps_dx.tile([P, KT, C], F32, name="dx_ps")
+            for kt in range(KT):
+                for which, (words, plane) in enumerate(((w1_w, w1_s), (w3_w, w3_s))):
+                    nc.tensor.matmul_mx(
+                        dx_ps[:, kt, :],
+                        lhsT=words[e][:, 0, kt * 256 : (kt + 1) * 256].bitcast(FP4X4),
+                        lhsT_scale=plane[:, e, kt * P : (kt + 1) * P],
+                        rhs=codes[:, which * C : (which + 1) * C].bitcast(FP8X4),
+                        rhs_scale=da_s[:, which * C : (which + 1) * C],
+                        start=(which == 0), stop=(which == 1),
+                    )
+            dx_sb[e] = work.tile([P, KT, C], F32, name="dx_sb", bufs=3)
+            nc.scalar.copy(dx_sb[e][:], dx_ps[:])
+            if e > 0:
+                scatter(e - 1)
+        scatter(E - 1)

@@ -21,6 +21,7 @@ P = 128
 PASSES = N // 512
 KT = K // P
 LIST_COLS = C // 16
+ON_VECTOR = 1
 
 
 def tile_moe_bdx_glu_silu_kernel(
@@ -29,13 +30,13 @@ def tile_moe_bdx_glu_silu_kernel(
     nc = tc.nc
     with ExitStack() as ctx:
         keep = ctx.enter_context(tc.tile_pool(name="keep", bufs=1))
-        work = ctx.enter_context(tc.tile_pool(name="work", bufs=2))
+        work = ctx.enter_context(tc.tile_pool(name="work", bufs=E))
         ps_dh = ctx.enter_context(tc.psum_pool(name="ps_dh", bufs=2))
         ps_tr = ctx.enter_context(tc.psum_pool(name="ps_tr", bufs=3))
-        ps_dx = ctx.enter_context(tc.psum_pool(name="ps_dx", bufs=2))
+        ps_dx = ctx.enter_context(tc.psum_pool(name="ps_dx", bufs=3))
 
         offsets = keep.tile([P, E * LIST_COLS], U16, name="offsets")
-        dy_w = keep.tile([P, PASSES, T], I32, name="dy_w", align_bytes=64)
+        dy_w = [keep.tile([P, T], I32, name="dy_w_%d" % s, align_bytes=64) for s in range(PASSES)]
         dy_s = keep.tile([P, PASSES, T], U8, name="dy_s", align_bytes=64)
         w2_s = keep.tile([P, E * PASSES, H], U8, name="w2_s", align_bytes=64)
         w1_s = keep.tile([P, E, K], U8, name="w1_s", align_bytes=64)
@@ -44,17 +45,13 @@ def tile_moe_bdx_glu_silu_kernel(
         gate_col = keep.tile([P, E], F32, name="gate_col")
         warm = keep.tile([P, 2], F32, name="warm")
 
-        for plane in (dy_s, w2_s, w1_s, w3_s):
-            nc.vector.memset(plane[:].rearrange("p a b -> p (a b)").bitcast(I32), 0)
-        nc.gpsimd.memset(warm[:, 0:1], 0.0)
-        nc.scalar.activation(warm[:, 1:2], warm[:, 0:1], ACT.Silu)
+        nc.vector.memset(dy_s[:].rearrange("p a b -> p (a b)").bitcast(I32), 0)
 
         def load_scales(queue, plane, rows):
             by_row = rows.rearrange("a (q r) n -> r q a n", r=4)
             for r in range(4):
                 queue.dma_start(out=plane[r:P:32, :, :].bitcast(I32), in_=by_row[r].bitcast(I32))
 
-        groups = [(0, 1), (1, 2), (2, 4)]
         w2_w, w1_w, w3_w, a1_t, a3_t = {}, {}, {}, {}, {}
 
         def load_words(name, table, src, lo, hi):
@@ -70,35 +67,36 @@ def tile_moe_bdx_glu_silu_kernel(
             for e in range(lo, hi):
                 table[e] = t[:, :, (e - lo) * C : (e - lo + 1) * C]
 
-        nc.sync.dma_start(offsets[:], offs)
-        nc.sync.dma_start(out=dy_w[:], in_=dy_words.rearrange("o p t d -> p o (t d)").bitcast(I32))
-        load_scales(nc.sync, dy_s, dy_scales)
-        load_words("w2", w2_w, w2_words, 0, 1)
-        load_saved("a1", a1_t, a1, 0, 1)
-        load_scales(nc.gpsimd, w2_s, w2_scales.rearrange("e s f n -> (e s) f n"))
-        with nc.allow_non_contiguous_dma(reason="one gate value to a partition"):
-            nc.gpsimd.dma_start(out=gate_col[:], in_=gate[0].rearrange("(e c) -> c e", e=E))
         make_identity(nc, ident[:])
-        load_saved("a3", a3_t, a3, 0, 1)
-        load_words("w2", w2_w, w2_words, 1, 2)
+        load_scales(nc.gpsimd, w3_s, w3_scales.rearrange("e s f n -> (e s) f n"))
+        nc.sync.dma_start(offsets[:], offs)
+        for s in range(PASSES):
+            nc.sync.dma_start(out=dy_w[s][:], in_=dy_words[s].rearrange("p t d -> p (t d)").bitcast(I32))
+        load_scales(nc.scalar, dy_s, dy_scales)
+        nc.vector.memset(warm[:, 0:1], 0.0)
+        nc.scalar.activation(warm[:, 1:2], warm[:, 0:1], ACT.Silu)
+        load_saved("a1", a1_t, a1, 0, 1)
+        load_words("w2", w2_w, w2_words, 0, 2)
+        load_scales(nc.sync, w2_s, w2_scales.rearrange("e s f n -> (e s) f n"))
         load_saved("a1", a1_t, a1, 1, 2)
+        with nc.allow_non_contiguous_dma(reason="one gate value to a partition"):
+            nc.sync.dma_start(out=gate_col[:], in_=gate[0].rearrange("(e c) -> c e", e=E))
+        load_saved("a3", a3_t, a3, 0, 2)
         load_words("w1", w1_w, w1_words, 0, 2)
         load_words("w3", w3_w, w3_words, 0, 2)
-        load_saved("a3", a3_t, a3, 1, 2)
         load_scales(nc.sync, w1_s, w1_scales.rearrange("e s f n -> (e s) f n"))
-        load_scales(nc.sync, w3_s, w3_scales.rearrange("e s f n -> (e s) f n"))
-        load_words("w2", w2_w, w2_words, 2, 4)
         load_saved("a1", a1_t, a1, 2, 4)
+        load_words("w2", w2_w, w2_words, 2, 4)
         load_saved("a3", a3_t, a3, 2, 4)
         load_words("w1", w1_w, w1_words, 2, 4)
         load_words("w3", w3_w, w3_words, 2, 4)
 
         g_w, g_s = {}, {}
-        for lo, hi in ((0, 1), (1, 4)):
+        for lo, hi in ((0, 2), (2, 4)):
             picks = offsets[:, lo * LIST_COLS : hi * LIST_COLS]
             for s in range(PASSES):
                 words = keep.tile([P, (hi - lo) * C], U32, name="g_w_%d_%d" % (lo, s), align_bytes=64)
-                nc.vector.tensor_copy(words[:], dy_w[:, s, :].bitcast(U32).indirect(picks))
+                nc.vector.tensor_copy(words[:], dy_w[s][:].bitcast(U32).indirect(picks))
                 for e in range(lo, hi):
                     g_w[e, s] = words[:, (e - lo) * C : (e - lo + 1) * C]
             for s in range(PASSES):
@@ -108,25 +106,28 @@ def tile_moe_bdx_glu_silu_kernel(
                     g_s[e, s] = scales[:, (e - lo) * C : (e - lo + 1) * C]
 
         windows = [keep.tile([P, T], F32, name="window_%d" % kt, align_bytes=64) for kt in range(KT)]
-        dx_sb = {}
-
-        def scatter(e):
-            picks = offsets[:, e * LIST_COLS : (e + 1) * LIST_COLS]
-            for kt in range(KT):
-                nc.vector.tensor_copy(windows[kt][:].indirect(picks), dx_sb[e][:, kt, :])
-                if e == E - 1:
-                    nc.sync.dma_start(out=out[kt * P : (kt + 1) * P, :], in_=windows[kt][:])
+        factor1, factor3, dh, dx_ps, dx_sb = {}, {}, {}, {}, {}
 
         def by_fours(ap):
             return ap.rearrange("p t (c i) -> p c t i", i=4)
 
-        for e in range(E):
+        def prepare(e):
             silu_neg = work.tile([P, 4, C], F32, name="silu_neg")
             nc.scalar.activation(silu_neg[:], a1_t[e], ACT.Silu, scale=-1.0)
             half_rest = work.tile([P, 4, C], F32, name="half_rest")
             nc.scalar.activation(half_rest[:], silu_neg[:], ACT.Copy, scale=-0.5, bias=0.5)
             tanh_half = work.tile([P, 4, C], F32, name="tanh_half")
             nc.scalar.activation(tanh_half[:], a1_t[e], ACT.Tanh, scale=0.5)
+            part = work.tile([P, 4, C], F32, name="part")
+            factor1[e] = work.tile([P, 4, C], F32, name="factor1")
+            if e < ON_VECTOR:
+                nc.vector.tensor_tensor(part[:], half_rest[:], a3_t[e], ALU.mult)
+                nc.vector.scalar_tensor_tensor(factor1[e][:], tanh_half[:], 1.0, part[:], ALU.add, ALU.mult)
+            else:
+                twice_sig = work.tile([P, 4, C], F32, name="twice_sig")
+                nc.scalar.activation(twice_sig[:], tanh_half[:], ACT.Copy, bias=1.0)
+                nc.gpsimd.tensor_tensor(part[:], half_rest[:], a3_t[e], ALU.mult)
+                nc.gpsimd.tensor_tensor(factor1[e][:], twice_sig[:], part[:], ALU.mult)
 
             dh_ps = ps_dh.tile([P, H], F32, name="dh_ps")
             for s in range(PASSES):
@@ -137,38 +138,55 @@ def tile_moe_bdx_glu_silu_kernel(
                 )
             dh_sb = work.tile([P, 4, P], F32, name="dh_sb", align_bytes=64)
             nc.scalar.activation(dh_sb[:], dh_ps[:].rearrange("c (p t) -> c t p", t=4), ACT.Copy, scale=gate_col[:, e : e + 1])
-            dh = ps_tr.tile([P, 4, C], F32, name="dh")
+            dh[e] = ps_tr.tile([P, 4, C], F32, name="dh")
             for t in range(4):
-                nc.tensor.transpose(dh[:, t, :], dh_sb[:, t, :], ident[:])
-            factor3 = work.tile([P, 4, C], F32, name="factor3")
-            nc.scalar.activation(factor3[:], a1_t[e], ACT.Silu)
+                nc.tensor.transpose(dh[e][:, t, :], dh_sb[:, t, :], ident[:])
+            factor3[e] = work.tile([P, 4, C], F32, name="factor3")
+            nc.scalar.activation(factor3[e][:], a1_t[e], ACT.Silu)
 
-            part = work.tile([P, 4, C], F32, name="part")
-            nc.vector.tensor_tensor(part[:], half_rest[:], a3_t[e], ALU.mult)
-            factor1 = work.tile([P, 4, C], F32, name="factor1")
-            nc.vector.scalar_tensor_tensor(factor1[:], tanh_half[:], 1.0, part[:], ALU.add, ALU.mult)
-            da = work.tile([P, 2, C, 4], BF16, name="da", align_bytes=64)
-            for which, factor in ((1, factor3), (0, factor1)):
+        def multiply(e):
+            if e == 2:
+                da = dx_sb[1][:].rearrange("p a b -> p (a b)").bitcast(BF16).rearrange("p (w j t) -> p w j t", w=2, t=4)
+            else:
+                da = work.tile([P, 2, C, 4], BF16, name="da", align_bytes=64)[:]
+            for which, factor in ((1, factor3[e]), (0, factor1[e])):
                 nc.vector.tensor_tensor(
-                    da[:, which].rearrange("p (c i) t -> p c t i", i=4), by_fours(dh[:]), by_fours(factor[:]), ALU.mult
+                    da[:, which].rearrange("p (c i) t -> p c t i", i=4), by_fours(dh[e][:]), by_fours(factor[:]), ALU.mult
                 )
             codes = work.tile([P, 2 * C], U32, name="codes", align_bytes=64)
             da_s = work.tile([P, 2 * C], U8, name="da_s", align_bytes=64)
-            nc.vector.quantize_mx(codes[:].bitcast(FP8X4), da_s[:], da[:].rearrange("p w j t -> p (w j t)"))
+            nc.vector.quantize_mx(codes[:].bitcast(FP8X4), da_s[:], da.rearrange("p w j t -> p (w j t)"))
 
-            dx_ps = ps_dx.tile([P, KT, C], F32, name="dx_ps")
+            dx_ps[e] = ps_dx.tile([P, KT, C], F32, name="dx_ps")
             for kt in range(KT):
                 for which, (words, plane) in enumerate(((w1_w, w1_s), (w3_w, w3_s))):
                     nc.tensor.matmul_mx(
-                        dx_ps[:, kt, :],
+                        dx_ps[e][:, kt, :],
                         lhsT=words[e][:, 0, kt * 256 : (kt + 1) * 256].bitcast(FP4X4),
                         lhsT_scale=plane[:, e, kt * P : (kt + 1) * P],
                         rhs=codes[:, which * C : (which + 1) * C].bitcast(FP8X4),
                         rhs_scale=da_s[:, which * C : (which + 1) * C],
                         start=(which == 0), stop=(which == 1),
                     )
-            dx_sb[e] = work.tile([P, KT, C], F32, name="dx_sb", bufs=3)
-            nc.scalar.copy(dx_sb[e][:], dx_ps[:])
-            if e > 0:
-                scatter(e - 1)
-        scatter(E - 1)
+
+        def scatter(e):
+            dx_sb[e] = factor3[E - 1] if e == E - 2 else work.tile([P, KT, C], F32, name="dx_sb", align_bytes=64)
+            nc.scalar.copy(dx_sb[e][:], dx_ps[e][:])
+            picks = offsets[:, e * LIST_COLS : (e + 1) * LIST_COLS]
+            for kt in range(KT):
+                nc.vector.tensor_copy(windows[kt][:].indirect(picks), dx_sb[e][:, kt, :])
+                if e == E - 1:
+                    nc.sync.dma_start(out=out[kt * P : (kt + 1) * P, :], in_=windows[kt][:])
+
+        prepare(0)
+        prepare(1)
+        multiply(0)
+        multiply(1)
+        scatter(0)
+        prepare(2)
+        scatter(1)
+        prepare(3)
+        multiply(2)
+        multiply(3)
+        scatter(2)
+        scatter(3)

@@ -21,7 +21,7 @@ P = 128
 PASSES = N // 512
 KT = K // P
 LIST_COLS = C // 16
-ON_VECTOR = 1
+ON_VECTOR = 2
 
 
 def tile_moe_bdx_glu_silu_kernel(
@@ -81,9 +81,10 @@ def tile_moe_bdx_glu_silu_kernel(
         load_saved("a1", a1_t, a1, 1, 2)
         with nc.allow_non_contiguous_dma(reason="one gate value to a partition"):
             nc.sync.dma_start(out=gate_col[:], in_=gate[0].rearrange("(e c) -> c e", e=E))
-        load_saved("a3", a3_t, a3, 0, 2)
+        load_saved("a3", a3_t, a3, 0, 1)
         load_words("w1", w1_w, w1_words, 0, 2)
         load_words("w3", w3_w, w3_words, 0, 2)
+        load_saved("a3", a3_t, a3, 1, 2)
         load_scales(nc.sync, w1_s, w1_scales.rearrange("e s f n -> (e s) f n"))
         load_saved("a1", a1_t, a1, 2, 4)
         load_words("w2", w2_w, w2_words, 2, 4)
@@ -108,17 +109,14 @@ def tile_moe_bdx_glu_silu_kernel(
         windows = [keep.tile([P, T], F32, name="window_%d" % kt, align_bytes=64) for kt in range(KT)]
         factor1, factor3, dh, dx_ps, dx_sb = {}, {}, {}, {}, {}
 
-        def by_fours(ap):
-            return ap.rearrange("p t (c i) -> p c t i", i=4)
+        def by_pairs(ap):
+            return ap.rearrange("p t (c i) -> p c t i", i=2)
 
-        def prepare(e):
-            silu_neg = work.tile([P, 4, C], F32, name="silu_neg")
-            nc.scalar.activation(silu_neg[:], a1_t[e], ACT.Silu, scale=-1.0)
-            half_rest = work.tile([P, 4, C], F32, name="half_rest")
-            nc.scalar.activation(half_rest[:], silu_neg[:], ACT.Copy, scale=-0.5, bias=0.5)
-            tanh_half = work.tile([P, 4, C], F32, name="tanh_half")
-            nc.scalar.activation(tanh_half[:], a1_t[e], ACT.Tanh, scale=0.5)
-            part = work.tile([P, 4, C], F32, name="part")
+        halves = {}
+
+        def combine(e):
+            half_rest, tanh_half = halves[e]
+            part = factor3[0] if e == 1 else work.tile([P, 4, C], F32, name="part")
             factor1[e] = work.tile([P, 4, C], F32, name="factor1")
             if e < ON_VECTOR:
                 nc.vector.tensor_tensor(part[:], half_rest[:], a3_t[e], ALU.mult)
@@ -128,6 +126,17 @@ def tile_moe_bdx_glu_silu_kernel(
                 nc.scalar.activation(twice_sig[:], tanh_half[:], ACT.Copy, bias=1.0)
                 nc.gpsimd.tensor_tensor(part[:], half_rest[:], a3_t[e], ALU.mult)
                 nc.gpsimd.tensor_tensor(factor1[e][:], twice_sig[:], part[:], ALU.mult)
+
+        def prepare(e):
+            silu_neg = work.tile([P, 4, C], F32, name="silu_neg")
+            nc.scalar.activation(silu_neg[:], a1_t[e], ACT.Silu, scale=-1.0)
+            half_rest = work.tile([P, 4, C], F32, name="half_rest")
+            nc.scalar.activation(half_rest[:], silu_neg[:], ACT.Copy, scale=-0.5, bias=0.5)
+            tanh_half = work.tile([P, 4, C], F32, name="tanh_half")
+            nc.scalar.activation(tanh_half[:], a1_t[e], ACT.Tanh, scale=0.5)
+            halves[e] = (half_rest, tanh_half)
+            if e != 1:
+                combine(e)
 
             dh_ps = ps_dh.tile([P, H], F32, name="dh_ps")
             for s in range(PASSES):
@@ -151,7 +160,7 @@ def tile_moe_bdx_glu_silu_kernel(
                 da = work.tile([P, 2, C, 4], BF16, name="da", align_bytes=64)[:]
             for which, factor in ((1, factor3[e]), (0, factor1[e])):
                 nc.vector.tensor_tensor(
-                    da[:, which].rearrange("p (c i) t -> p c t i", i=4), by_fours(dh[e][:]), by_fours(factor[:]), ALU.mult
+                    da[:, which].rearrange("p (c i) t -> p c t i", i=2), by_pairs(dh[e][:]), by_pairs(factor[:]), ALU.mult
                 )
             codes = work.tile([P, 2 * C], U32, name="codes", align_bytes=64)
             da_s = work.tile([P, 2 * C], U8, name="da_s", align_bytes=64)
@@ -181,6 +190,7 @@ def tile_moe_bdx_glu_silu_kernel(
         prepare(0)
         prepare(1)
         multiply(0)
+        combine(1)
         multiply(1)
         scatter(0)
         prepare(2)

@@ -47,9 +47,9 @@ def tile_moe_bdx_glu_silu_kernel(
 
         nc.vector.memset(dy_s[:].rearrange("p a b -> p (a b)").bitcast(I32), 0)
 
-        def load_scales(queue, plane, rows):
+        def load_scales(queue, plane, rows, lo=0, hi=4):
             by_row = rows.rearrange("a (q r) n -> r q a n", r=4)
-            for r in range(4):
+            for r in range(lo, hi):
                 queue.dma_start(out=plane[r:P:32, :, :].bitcast(I32), in_=by_row[r].bitcast(I32))
 
         w2_w, w1_w, w3_w, a1_t, a3_t = {}, {}, {}, {}, {}
@@ -85,9 +85,10 @@ def tile_moe_bdx_glu_silu_kernel(
         load_words("w1", w1_w, w1_words, 0, 2)
         load_words("w3", w3_w, w3_words, 0, 2)
         load_saved("a3", a3_t, a3, 1, 2)
-        load_scales(nc.sync, w1_s, w1_scales.rearrange("e s f n -> (e s) f n"))
-        load_saved("a1", a1_t, a1, 2, 4)
         load_words("w2", w2_w, w2_words, 2, 4)
+        load_scales(nc.sync, w1_s, w1_scales.rearrange("e s f n -> (e s) f n"), 0, 3)
+        load_saved("a1", a1_t, a1, 2, 4)
+        load_scales(nc.sync, w1_s, w1_scales.rearrange("e s f n -> (e s) f n"), 3, 4)
         load_saved("a3", a3_t, a3, 2, 4)
         load_words("w1", w1_w, w1_words, 2, 4)
         load_words("w3", w3_w, w3_words, 2, 4)
@@ -150,15 +151,15 @@ def tile_moe_bdx_glu_silu_kernel(
             dh[e] = ps_tr.tile([P, 4, C], F32, name="dh")
             for t in range(4):
                 nc.tensor.transpose(dh[e][:, t, :], dh_sb[:, t, :], ident[:])
-            factor3[e] = work.tile([P, 4, C], F32, name="factor3")
+            factor3[e] = work.tile([P, 4, C], F32, name="factor3", align_bytes=64)
             nc.scalar.activation(factor3[e][:], a1_t[e], ACT.Silu)
 
         def multiply(e):
-            if e == 2:
+            if e == 3:
                 da = dx_sb[1][:].rearrange("p a b -> p (a b)").bitcast(BF16).rearrange("p (w j t) -> p w j t", w=2, t=4)
             else:
                 da = work.tile([P, 2, C, 4], BF16, name="da", align_bytes=64)[:]
-            for which, factor in ((1, factor3[e]), (0, factor1[e])):
+            for which, factor in enumerate((factor3[e], factor1[e])):
                 nc.vector.tensor_tensor(
                     da[:, which].rearrange("p (c i) t -> p c t i", i=2), by_pairs(dh[e][:]), by_pairs(factor[:]), ALU.mult
                 )
@@ -168,7 +169,7 @@ def tile_moe_bdx_glu_silu_kernel(
 
             dx_ps[e] = ps_dx.tile([P, KT, C], F32, name="dx_ps")
             for kt in range(KT):
-                for which, (words, plane) in enumerate(((w1_w, w1_s), (w3_w, w3_s))):
+                for which, (words, plane) in enumerate(((w3_w, w3_s), (w1_w, w1_s))):
                     nc.tensor.matmul_mx(
                         dx_ps[e][:, kt, :],
                         lhsT=words[e][:, 0, kt * 256 : (kt + 1) * 256].bitcast(FP4X4),
@@ -179,7 +180,7 @@ def tile_moe_bdx_glu_silu_kernel(
                     )
 
         def scatter(e):
-            dx_sb[e] = factor3[E - 1] if e == E - 2 else work.tile([P, KT, C], F32, name="dx_sb", align_bytes=64)
+            dx_sb[e] = factor3[e + 1] if e in (1, 2) else work.tile([P, KT, C], F32, name="dx_sb", align_bytes=64)
             nc.scalar.copy(dx_sb[e][:], dx_ps[e][:])
             picks = offsets[:, e * LIST_COLS : (e + 1) * LIST_COLS]
             for kt in range(KT):
@@ -194,9 +195,9 @@ def tile_moe_bdx_glu_silu_kernel(
         multiply(1)
         scatter(0)
         prepare(2)
+        multiply(2)
         scatter(1)
         prepare(3)
-        multiply(2)
         multiply(3)
         scatter(2)
         scatter(3)

@@ -21,7 +21,6 @@ P = 128
 PASSES = N // 512
 KT = K // P
 LIST_COLS = C // 16
-ON_VECTOR = 2
 
 
 def tile_moe_bdx_glu_silu_kernel(
@@ -31,6 +30,7 @@ def tile_moe_bdx_glu_silu_kernel(
     with ExitStack() as ctx:
         keep = ctx.enter_context(tc.tile_pool(name="keep", bufs=1))
         work = ctx.enter_context(tc.tile_pool(name="work", bufs=E))
+        picked = ctx.enter_context(tc.tile_pool(name="picked", bufs=E - 1))
         ps_dh = ctx.enter_context(tc.psum_pool(name="ps_dh", bufs=2))
         ps_tr = ctx.enter_context(tc.psum_pool(name="ps_tr", bufs=3))
         ps_dx = ctx.enter_context(tc.psum_pool(name="ps_dx", bufs=3))
@@ -43,9 +43,7 @@ def tile_moe_bdx_glu_silu_kernel(
         w3_s = keep.tile([P, E, K], U8, name="w3_s", align_bytes=64)
         ident = keep.tile([P, P], F32, name="ident", align_bytes=64)
         gate_col = keep.tile([P, E], F32, name="gate_col")
-        warm = keep.tile([P, 2], F32, name="warm")
-
-        nc.vector.memset(dy_s[:].rearrange("p a b -> p (a b)").bitcast(I32), 0)
+        gate_half = keep.tile([P, E], F32, name="gate_half")
 
         def load_scales(queue, plane, rows, lo=0, hi=4):
             by_row = rows.rearrange("a (q r) n -> r q a n", r=4)
@@ -57,7 +55,8 @@ def tile_moe_bdx_glu_silu_kernel(
         def load_words(name, table, src, lo, hi):
             passes = src.shape[1]
             t = keep.tile([P, (hi - lo) * passes, 1024], U8, name="%s_%d" % (name, lo), align_bytes=64)
-            nc.sync.dma_start(out=t[:].bitcast(I32), in_=src[lo:hi].rearrange("e s p b -> p (e s) b").bitcast(I32))
+            rows = src.rearrange("e s p b -> p (e s) b").bitcast(I32)
+            nc.sync.dma_start(out=t[:].bitcast(I32), in_=rows[:, lo * passes : hi * passes, :])
             for e in range(lo, hi):
                 table[e] = t[:, (e - lo) * passes : (e - lo + 1) * passes, :]
 
@@ -67,111 +66,94 @@ def tile_moe_bdx_glu_silu_kernel(
             for e in range(lo, hi):
                 table[e] = t[:, :, (e - lo) * C : (e - lo + 1) * C]
 
+        nc.gpsimd.memset(dy_s[:].rearrange("p a b -> p (a b)").bitcast(I32), 0)
         make_identity(nc, ident[:])
-        load_scales(nc.gpsimd, w3_s, w3_scales.rearrange("e s f n -> (e s) f n"))
         nc.sync.dma_start(offsets[:], offs)
+        load_scales(nc.scalar, dy_s, dy_scales, 0, 2)
+        load_scales(nc.sync, dy_s, dy_scales, 2, 4)
+        load_saved("a1", a1_t, a1, 0, 2)
         for s in range(PASSES):
             nc.sync.dma_start(out=dy_w[s][:], in_=dy_words[s].rearrange("p t d -> p (t d)").bitcast(I32))
-        load_scales(nc.scalar, dy_s, dy_scales)
-        nc.vector.memset(warm[:, 0:1], 0.0)
-        nc.scalar.activation(warm[:, 1:2], warm[:, 0:1], ACT.Silu)
-        load_saved("a1", a1_t, a1, 0, 1)
-        load_words("w2", w2_w, w2_words, 0, 2)
+        load_words("w2", w2_w, w2_words, 0, 1)
         load_scales(nc.sync, w2_s, w2_scales.rearrange("e s f n -> (e s) f n"))
-        load_saved("a1", a1_t, a1, 1, 2)
         with nc.allow_non_contiguous_dma(reason="one gate value to a partition"):
             nc.sync.dma_start(out=gate_col[:], in_=gate[0].rearrange("(e c) -> c e", e=E))
-        load_saved("a3", a3_t, a3, 0, 1)
-        load_words("w1", w1_w, w1_words, 0, 2)
-        load_words("w3", w3_w, w3_words, 0, 2)
-        load_saved("a3", a3_t, a3, 1, 2)
-        load_words("w2", w2_w, w2_words, 2, 4)
-        load_scales(nc.sync, w1_s, w1_scales.rearrange("e s f n -> (e s) f n"), 0, 3)
+        w1_rows = w1_scales.rearrange("e s f n -> (e s) f n")
+        w3_rows = w3_scales.rearrange("e s f n -> (e s) f n")
         load_saved("a1", a1_t, a1, 2, 4)
-        load_scales(nc.sync, w1_s, w1_scales.rearrange("e s f n -> (e s) f n"), 3, 4)
-        load_saved("a3", a3_t, a3, 2, 4)
-        load_words("w1", w1_w, w1_words, 2, 4)
-        load_words("w3", w3_w, w3_words, 2, 4)
+        load_scales(nc.sync, w3_s, w3_rows, 0, 2)
+        load_saved("a3", a3_t, a3, 0, 2)
+        load_scales(nc.sync, w3_s, w3_rows, 2, 4)
+        load_words("w2", w2_w, w2_words, 1, 2)
+        load_scales(nc.sync, w1_s, w1_rows, 0, 2)
+        load_words("w1", w1_w, w1_words, 0, 1)
+        load_scales(nc.sync, w1_s, w1_rows, 2, 4)
+        load_words("w2", w2_w, w2_words, 2, 4)
+        load_words("w3", w3_w, w3_words, 0, 1)
+        load_saved("a3", a3_t, a3, 2, 3)
+        load_words("w1", w1_w, w1_words, 1, 4)
+        load_words("w3", w3_w, w3_words, 1, 4)
+        load_saved("a3", a3_t, a3, 3, 4)
 
         g_w, g_s = {}, {}
-        for lo, hi in ((0, 2), (2, 4)):
-            picks = offsets[:, lo * LIST_COLS : hi * LIST_COLS]
+
+        def gather(e):
+            picks = offsets[:, e * LIST_COLS : (e + 1) * LIST_COLS]
             for s in range(PASSES):
-                words = keep.tile([P, (hi - lo) * C], U32, name="g_w_%d_%d" % (lo, s), align_bytes=64)
-                nc.vector.tensor_copy(words[:], dy_w[s][:].bitcast(U32).indirect(picks))
-                for e in range(lo, hi):
-                    g_w[e, s] = words[:, (e - lo) * C : (e - lo + 1) * C]
+                g_s[e, s] = picked.tile([P, C], U8, name="g_s_%d" % s, align_bytes=64)
+                nc.vector.tensor_copy(g_s[e, s][:], dy_s[:, s, :].indirect(picks))
             for s in range(PASSES):
-                scales = keep.tile([P, (hi - lo) * C], U8, name="g_s_%d_%d" % (lo, s), align_bytes=64)
-                nc.vector.tensor_copy(scales[:], dy_s[:, s, :].indirect(picks))
-                for e in range(lo, hi):
-                    g_s[e, s] = scales[:, (e - lo) * C : (e - lo + 1) * C]
+                g_w[e, s] = picked.tile([P, C], U32, name="g_w_%d" % s, align_bytes=64)
+                nc.vector.tensor_copy(g_w[e, s][:], dy_w[s][:].bitcast(U32).indirect(picks))
 
         windows = [keep.tile([P, T], F32, name="window_%d" % kt, align_bytes=64) for kt in range(KT)]
-        factor1, factor3, dh, dx_ps, dx_sb = {}, {}, {}, {}, {}
+        ring = keep.tile([P, KT + 2, C], F32, name="ring", align_bytes=64)
+        tanh_half, silu_neg, slope, dh, dx_ps, dx_sb = {}, {}, {}, {}, {}, {}
 
         def by_pairs(ap):
             return ap.rearrange("p t (c i) -> p c t i", i=2)
 
-        halves = {}
+        def functions(e):
+            tanh_half[e] = work.tile([P, 4, C], F32, name="tanh_half", align_bytes=64)
+            nc.scalar.activation(tanh_half[e][:], a1_t[e], ACT.Tanh, scale=0.5)
+            silu_neg[e] = work.tile([P, 4, C], F32, name="silu_neg", align_bytes=64)
+            nc.scalar.activation(silu_neg[e][:], a1_t[e], ACT.Silu, scale=-1.0)
 
-        def combine(e):
-            half_rest, tanh_half = halves[e]
-            part = factor3[0] if e == 1 else work.tile([P, 4, C], F32, name="part")
-            factor1[e] = work.tile([P, 4, C], F32, name="factor1")
-            if e < ON_VECTOR:
-                nc.vector.tensor_tensor(part[:], half_rest[:], a3_t[e], ALU.mult)
-                nc.vector.scalar_tensor_tensor(factor1[e][:], tanh_half[:], 1.0, part[:], ALU.add, ALU.mult)
-            else:
-                twice_sig = work.tile([P, 4, C], F32, name="twice_sig")
-                nc.scalar.activation(twice_sig[:], tanh_half[:], ACT.Copy, bias=1.0)
-                nc.gpsimd.tensor_tensor(part[:], half_rest[:], a3_t[e], ALU.mult)
-                nc.gpsimd.tensor_tensor(factor1[e][:], twice_sig[:], part[:], ALU.mult)
-
-        def prepare(e):
-            silu_neg = work.tile([P, 4, C], F32, name="silu_neg")
-            nc.scalar.activation(silu_neg[:], a1_t[e], ACT.Silu, scale=-1.0)
-            half_rest = work.tile([P, 4, C], F32, name="half_rest")
-            nc.scalar.activation(half_rest[:], silu_neg[:], ACT.Copy, scale=-0.5, bias=0.5)
-            tanh_half = work.tile([P, 4, C], F32, name="tanh_half")
-            nc.scalar.activation(tanh_half[:], a1_t[e], ACT.Tanh, scale=0.5)
-            halves[e] = (half_rest, tanh_half)
-            if e != 1:
-                combine(e)
-
+        def first_product(e):
             dh_ps = ps_dh.tile([P, H], F32, name="dh_ps")
             for s in range(PASSES):
                 nc.tensor.matmul_mx(
-                    dh_ps[:], lhsT=g_w[e, s].bitcast(FP8X4), lhsT_scale=g_s[e, s],
+                    dh_ps[:], lhsT=g_w[e, s][:].bitcast(FP8X4), lhsT_scale=g_s[e, s][:],
                     rhs=w2_w[e][:, s, :].bitcast(FP4X4), rhs_scale=w2_s[:, e * PASSES + s, :],
                     start=(s == 0), stop=(s == PASSES - 1),
                 )
             dh_sb = work.tile([P, 4, P], F32, name="dh_sb", align_bytes=64)
-            nc.scalar.activation(dh_sb[:], dh_ps[:].rearrange("c (p t) -> c t p", t=4), ACT.Copy, scale=gate_col[:, e : e + 1])
+            nc.scalar.activation(dh_sb[:], dh_ps[:].rearrange("c (p t) -> c t p", t=4), ACT.Copy, scale=gate_half[:, e : e + 1])
             dh[e] = ps_tr.tile([P, 4, C], F32, name="dh")
             for t in range(4):
                 nc.tensor.transpose(dh[e][:, t, :], dh_sb[:, t, :], ident[:])
-            factor3[e] = work.tile([P, 4, C], F32, name="factor3", align_bytes=64)
-            nc.scalar.activation(factor3[e][:], a1_t[e], ACT.Silu)
 
         def multiply(e):
-            if e == 3:
-                da = dx_sb[1][:].rearrange("p a b -> p (a b)").bitcast(BF16).rearrange("p (w j t) -> p w j t", w=2, t=4)
-            else:
-                da = work.tile([P, 2, C, 4], BF16, name="da", align_bytes=64)[:]
-            for which, factor in enumerate((factor3[e], factor1[e])):
-                nc.vector.tensor_tensor(
-                    da[:, which].rearrange("p (c i) t -> p c t i", i=2), by_pairs(dh[e][:]), by_pairs(factor[:]), ALU.mult
-                )
+            sig_dh = work.tile([P, 4, C], F32, name="sig_dh", align_bytes=64)
+            nc.vector.scalar_tensor_tensor(sig_dh[:], tanh_half[e][:], 1.0, dh[e][:], ALU.add, ALU.mult)
+            slope[e] = work.tile([P, 4, C], F32, name="slope", align_bytes=64)
+            nc.vector.scalar_tensor_tensor(slope[e][:], silu_neg[e][:], 1.0, a3_t[e], ALU.subtract, ALU.mult)
+            da = work.tile([P, 2, C, 4], BF16, name="da", align_bytes=64)
+            nc.vector.tensor_tensor(
+                da[:, 0].rearrange("p (c i) t -> p c t i", i=2), by_pairs(sig_dh[:]), by_pairs(a1_t[e]), ALU.mult
+            )
+            nc.vector.scalar_tensor_tensor(
+                da[:, 1], sig_dh[:].rearrange("p t c -> p c t"), -1.0, slope[e][:].rearrange("p t c -> p c t"), ALU.mult, ALU.mult
+            )
             codes = work.tile([P, 2 * C], U32, name="codes", align_bytes=64)
             da_s = work.tile([P, 2 * C], U8, name="da_s", align_bytes=64)
-            nc.vector.quantize_mx(codes[:].bitcast(FP8X4), da_s[:], da.rearrange("p w j t -> p (w j t)"))
+            nc.vector.quantize_mx(codes[:].bitcast(FP8X4), da_s[:], da[:].rearrange("p w j t -> p (w j t)"))
 
-            dx_ps[e] = ps_dx.tile([P, KT, C], F32, name="dx_ps")
+            dx_ps[e] = [ps_dx.tile([P, 2, C], F32, name="dx_ps") for half in range(2)] if e == E - 1 else ps_dx.tile([P, KT, C], F32, name="dx_ps")
             for kt in range(KT):
                 for which, (words, plane) in enumerate(((w3_w, w3_s), (w1_w, w1_s))):
                     nc.tensor.matmul_mx(
-                        dx_ps[e][:, kt, :],
+                        dx_ps[e][kt // 2][:, kt % 2, :] if e == E - 1 else dx_ps[e][:, kt, :],
                         lhsT=words[e][:, 0, kt * 256 : (kt + 1) * 256].bitcast(FP4X4),
                         lhsT_scale=plane[:, e, kt * P : (kt + 1) * P],
                         rhs=codes[:, which * C : (which + 1) * C].bitcast(FP8X4),
@@ -179,25 +161,42 @@ def tile_moe_bdx_glu_silu_kernel(
                         start=(which == 0), stop=(which == 1),
                     )
 
-        def scatter(e):
-            dx_sb[e] = factor3[e + 1] if e in (1, 2) else work.tile([P, KT, C], F32, name="dx_sb", align_bytes=64)
-            nc.scalar.copy(dx_sb[e][:], dx_ps[e][:])
+        def scatter(e, kt, on_scalar):
             picks = offsets[:, e * LIST_COLS : (e + 1) * LIST_COLS]
-            for kt in range(KT):
+            if on_scalar:
+                nc.scalar.activation(windows[kt][:].indirect(picks), dx_sb[e][:, kt, :], ACT.Copy)
+            else:
                 nc.vector.tensor_copy(windows[kt][:].indirect(picks), dx_sb[e][:, kt, :])
-                if e == E - 1:
-                    nc.sync.dma_start(out=out[kt * P : (kt + 1) * P, :], in_=windows[kt][:])
+            if e == E - 1:
+                nc.sync.dma_start(out=out[kt * P : (kt + 1) * P, :], in_=windows[kt][:])
 
-        prepare(0)
-        prepare(1)
+        for e in range(E - 1):
+            gather(e)
+        nc.vector.tensor_scalar(gate_half[:], gate_col[:], 0.5, None, ALU.mult)
+        functions(0)
+        first_product(0)
+        gather(3)
+        for e in range(1, E):
+            functions(e)
+            first_product(e)
         multiply(0)
-        combine(1)
         multiply(1)
-        scatter(0)
-        prepare(2)
+        dx_sb[0] = ring[:, 0:KT, :]
+        nc.scalar.copy(dx_sb[0], dx_ps[0][:])
+        for kt in reversed(range(KT)):
+            scatter(0, kt, True)
         multiply(2)
-        scatter(1)
-        prepare(3)
+        dx_sb[1] = ring[:, 2 : KT + 2, :]
+        nc.scalar.copy(dx_sb[1], dx_ps[1][:])
+        for kt in range(KT):
+            scatter(1, kt, True)
         multiply(3)
-        scatter(2)
-        scatter(3)
+        dx_sb[2] = slope[3][:]
+        nc.vector.tensor_copy(dx_sb[2], dx_ps[2][:])
+        for kt in range(KT):
+            scatter(2, kt, False)
+        dx_sb[3] = work.tile([P, KT, C], F32, name="dx_sb", align_bytes=64)[:]
+        nc.vector.tensor_copy(dx_sb[3][:, 0:2, :], dx_ps[3][0][:])
+        nc.scalar.copy(dx_sb[3][:, 2:4, :], dx_ps[3][1][:])
+        for kt in (0, 2, 1, 3):
+            scatter(3, kt, kt >= 2)

@@ -30,19 +30,19 @@ def tile_moe_bdx_glu_silu_kernel(
     with ExitStack() as ctx:
         keep = ctx.enter_context(tc.tile_pool(name="keep", bufs=1))
         work = ctx.enter_context(tc.tile_pool(name="work", bufs=E))
-        picked = ctx.enter_context(tc.tile_pool(name="picked", bufs=E - 1))
+        reused = ctx.enter_context(tc.tile_pool(name="reused", bufs=1))
         ps_dh = ctx.enter_context(tc.psum_pool(name="ps_dh", bufs=2))
         ps_tr = ctx.enter_context(tc.psum_pool(name="ps_tr", bufs=3))
         ps_dx = ctx.enter_context(tc.psum_pool(name="ps_dx", bufs=3))
 
         offsets = keep.tile([P, E * LIST_COLS], U16, name="offsets")
-        dy_w = [keep.tile([P, T], I32, name="dy_w_%d" % s, align_bytes=64) for s in range(PASSES)]
+        dy_w = keep.tile([P, PASSES, T], I32, name="dy_w", align_bytes=64)
         dy_s = keep.tile([P, PASSES, T], U8, name="dy_s", align_bytes=64)
         w2_s = keep.tile([P, E * PASSES, H], U8, name="w2_s", align_bytes=64)
         w1_s = keep.tile([P, E, K], U8, name="w1_s", align_bytes=64)
         w3_s = keep.tile([P, E, K], U8, name="w3_s", align_bytes=64)
         ident = keep.tile([P, P], F32, name="ident", align_bytes=64)
-        gate_col = keep.tile([P, E], F32, name="gate_col")
+        gate_rows = keep.tile([P, C], F32, name="gate_rows", align_bytes=64)
         gate_half = keep.tile([P, E], F32, name="gate_half")
 
         def load_scales(queue, plane, rows, lo=0, hi=4):
@@ -54,7 +54,10 @@ def tile_moe_bdx_glu_silu_kernel(
 
         def load_words(name, table, src, lo, hi):
             passes = src.shape[1]
-            t = keep.tile([P, (hi - lo) * passes, 1024], U8, name="%s_%d" % (name, lo), align_bytes=64)
+            if name == "w2" and lo == E - 1:
+                t = reused.tile([P, passes, 1024], U8, name="w2_last", align_bytes=64, offset=0)
+            else:
+                t = keep.tile([P, (hi - lo) * passes, 1024], U8, name="%s_%d" % (name, lo), align_bytes=64)
             rows = src.rearrange("e s p b -> p (e s) b").bitcast(I32)
             nc.sync.dma_start(out=t[:].bitcast(I32), in_=rows[:, lo * passes : hi * passes, :])
             for e in range(lo, hi):
@@ -67,28 +70,28 @@ def tile_moe_bdx_glu_silu_kernel(
                 table[e] = t[:, :, (e - lo) * C : (e - lo + 1) * C]
 
         nc.gpsimd.memset(dy_s[:].rearrange("p a b -> p (a b)").bitcast(I32), 0)
+        nc.gpsimd.memset(gate_rows[:], 0.0)
         make_identity(nc, ident[:])
         nc.sync.dma_start(offsets[:], offs)
         load_scales(nc.scalar, dy_s, dy_scales, 0, 2)
-        load_scales(nc.sync, dy_s, dy_scales, 2, 4)
         load_saved("a1", a1_t, a1, 0, 2)
-        for s in range(PASSES):
-            nc.sync.dma_start(out=dy_w[s][:], in_=dy_words[s].rearrange("p t d -> p (t d)").bitcast(I32))
+        load_scales(nc.sync, dy_s, dy_scales, 2, 4)
+        nc.sync.dma_start(out=dy_w[:], in_=dy_words.rearrange("s p t d -> p s (t d)").bitcast(I32))
         load_words("w2", w2_w, w2_words, 0, 1)
         load_scales(nc.sync, w2_s, w2_scales.rearrange("e s f n -> (e s) f n"))
-        with nc.allow_non_contiguous_dma(reason="one gate value to a partition"):
-            nc.sync.dma_start(out=gate_col[:], in_=gate[0].rearrange("(e c) -> c e", e=E))
+        nc.sync.dma_start(out=gate_rows[0:E, :], in_=gate[0].rearrange("(e c) -> e c", e=E))
         w1_rows = w1_scales.rearrange("e s f n -> (e s) f n")
         w3_rows = w3_scales.rearrange("e s f n -> (e s) f n")
-        load_saved("a1", a1_t, a1, 2, 4)
-        load_scales(nc.sync, w3_s, w3_rows, 0, 2)
         load_saved("a3", a3_t, a3, 0, 2)
-        load_scales(nc.sync, w3_s, w3_rows, 2, 4)
+        load_scales(nc.sync, w3_s, w3_rows, 0, 2)
         load_words("w2", w2_w, w2_words, 1, 2)
+        load_scales(nc.sync, w3_s, w3_rows, 2, 4)
+        load_saved("a1", a1_t, a1, 2, 4)
         load_scales(nc.sync, w1_s, w1_rows, 0, 2)
         load_words("w1", w1_w, w1_words, 0, 1)
         load_scales(nc.sync, w1_s, w1_rows, 2, 4)
-        load_words("w2", w2_w, w2_words, 2, 4)
+        load_words("w2", w2_w, w2_words, 2, 3)
+        load_words("w2", w2_w, w2_words, 3, 4)
         load_words("w3", w3_w, w3_words, 0, 1)
         load_saved("a3", a3_t, a3, 2, 3)
         load_words("w1", w1_w, w1_words, 1, 4)
@@ -97,33 +100,41 @@ def tile_moe_bdx_glu_silu_kernel(
 
         g_w, g_s = {}, {}
 
-        def gather(e):
-            picks = offsets[:, e * LIST_COLS : (e + 1) * LIST_COLS]
+        def gather(lo, hi, tag):
+            picks = offsets[:, lo * LIST_COLS : hi * LIST_COLS]
             for s in range(PASSES):
-                g_s[e, s] = picked.tile([P, C], U8, name="g_s_%d" % s, align_bytes=64)
-                nc.vector.tensor_copy(g_s[e, s][:], dy_s[:, s, :].indirect(picks))
+                scales = keep.tile([P, (hi - lo) * C], U8, name="g_s_%s_%d" % (tag, s), align_bytes=64)
+                nc.vector.tensor_copy(scales[:], dy_s[:, s, :].indirect(picks))
+                for e in range(lo, hi):
+                    g_s[e, s] = scales[:, (e - lo) * C : (e - lo + 1) * C]
             for s in range(PASSES):
-                g_w[e, s] = picked.tile([P, C], U32, name="g_w_%d" % s, align_bytes=64)
-                nc.vector.tensor_copy(g_w[e, s][:], dy_w[s][:].bitcast(U32).indirect(picks))
+                words = keep.tile([P, (hi - lo) * C], U32, name="g_w_%s_%d" % (tag, s), align_bytes=64)
+                nc.vector.tensor_copy(words[:], dy_w[:, s, :].bitcast(U32).indirect(picks))
+                for e in range(lo, hi):
+                    g_w[e, s] = words[:, (e - lo) * C : (e - lo + 1) * C]
 
         windows = [keep.tile([P, T], F32, name="window_%d" % kt, align_bytes=64) for kt in range(KT)]
-        ring = keep.tile([P, KT + 2, C], F32, name="ring", align_bytes=64)
+        ring = reused.tile([P, KT + 2, C], F32, name="ring", align_bytes=64, offset=0)
         tanh_half, silu_neg, slope, dh, dx_ps, dx_sb = {}, {}, {}, {}, {}, {}
 
         def by_pairs(ap):
             return ap.rearrange("p t (c i) -> p c t i", i=2)
 
         def functions(e):
-            tanh_half[e] = work.tile([P, 4, C], F32, name="tanh_half", align_bytes=64)
-            nc.scalar.activation(tanh_half[e][:], a1_t[e], ACT.Tanh, scale=0.5)
             silu_neg[e] = work.tile([P, 4, C], F32, name="silu_neg", align_bytes=64)
             nc.scalar.activation(silu_neg[e][:], a1_t[e], ACT.Silu, scale=-1.0)
+            tanh_half[e] = work.tile([P, 4, C], F32, name="tanh_half", align_bytes=64)
+            nc.scalar.activation(tanh_half[e][:], a1_t[e], ACT.Tanh, scale=0.5)
+            rest = work.tile([P, 4, C], F32, name="rest", align_bytes=64)
+            nc.gpsimd.tensor_scalar(rest[:], silu_neg[e][:], -1.0, 1.0, ALU.mult, ALU.add)
+            slope[e] = work.tile([P, 4, C], F32, name="slope", align_bytes=64)
+            nc.gpsimd.tensor_tensor(slope[e][:], rest[:], a3_t[e], ALU.mult)
 
         def first_product(e):
             dh_ps = ps_dh.tile([P, H], F32, name="dh_ps")
             for s in range(PASSES):
                 nc.tensor.matmul_mx(
-                    dh_ps[:], lhsT=g_w[e, s][:].bitcast(FP8X4), lhsT_scale=g_s[e, s][:],
+                    dh_ps[:], lhsT=g_w[e, s].bitcast(FP8X4), lhsT_scale=g_s[e, s],
                     rhs=w2_w[e][:, s, :].bitcast(FP4X4), rhs_scale=w2_s[:, e * PASSES + s, :],
                     start=(s == 0), stop=(s == PASSES - 1),
                 )
@@ -136,15 +147,11 @@ def tile_moe_bdx_glu_silu_kernel(
         def multiply(e):
             sig_dh = work.tile([P, 4, C], F32, name="sig_dh", align_bytes=64)
             nc.vector.scalar_tensor_tensor(sig_dh[:], tanh_half[e][:], 1.0, dh[e][:], ALU.add, ALU.mult)
-            slope[e] = work.tile([P, 4, C], F32, name="slope", align_bytes=64)
-            nc.vector.scalar_tensor_tensor(slope[e][:], silu_neg[e][:], 1.0, a3_t[e], ALU.subtract, ALU.mult)
             da = work.tile([P, 2, C, 4], BF16, name="da", align_bytes=64)
-            nc.vector.tensor_tensor(
-                da[:, 0].rearrange("p (c i) t -> p c t i", i=2), by_pairs(sig_dh[:]), by_pairs(a1_t[e]), ALU.mult
-            )
-            nc.vector.scalar_tensor_tensor(
-                da[:, 1], sig_dh[:].rearrange("p t c -> p c t"), -1.0, slope[e][:].rearrange("p t c -> p c t"), ALU.mult, ALU.mult
-            )
+            for which, factor in enumerate((a1_t[e], slope[e][:])):
+                nc.vector.tensor_tensor(
+                    da[:, which].rearrange("p (c i) t -> p c t i", i=2), by_pairs(sig_dh[:]), by_pairs(factor), ALU.mult
+                )
             codes = work.tile([P, 2 * C], U32, name="codes", align_bytes=64)
             da_s = work.tile([P, 2 * C], U8, name="da_s", align_bytes=64)
             nc.vector.quantize_mx(codes[:].bitcast(FP8X4), da_s[:], da[:].rearrange("p w j t -> p (w j t)"))
@@ -170,16 +177,21 @@ def tile_moe_bdx_glu_silu_kernel(
             if e == E - 1:
                 nc.sync.dma_start(out=out[kt * P : (kt + 1) * P, :], in_=windows[kt][:])
 
-        for e in range(E - 1):
-            gather(e)
-        nc.vector.tensor_scalar(gate_half[:], gate_col[:], 0.5, None, ALU.mult)
+        gather(0, 1, "outer")
+        gather(1, 3, "inner")
+        gate_ps = ps_tr.tile([P, 4, C], F32, name="dh")
+        nc.tensor.transpose(gate_ps[:, 0, :], gate_rows[:], ident[:])
+        nc.scalar.activation(gate_half[:], gate_ps[:, 0, 0:E], ACT.Copy, scale=0.5)
         functions(0)
         first_product(0)
-        gather(3)
-        for e in range(1, E):
-            functions(e)
-            first_product(e)
+        gather(3, 4, "outer")
+        functions(1)
+        first_product(1)
         multiply(0)
+        for e in range(2, E):
+            functions(e)
+        for e in range(2, E):
+            first_product(e)
         multiply(1)
         dx_sb[0] = ring[:, 0:KT, :]
         nc.scalar.copy(dx_sb[0], dx_ps[0][:])
@@ -188,12 +200,15 @@ def tile_moe_bdx_glu_silu_kernel(
         multiply(2)
         dx_sb[1] = ring[:, 2 : KT + 2, :]
         nc.scalar.copy(dx_sb[1], dx_ps[1][:])
-        for kt in range(KT):
+        for kt in (0, 1):
             scatter(1, kt, True)
         multiply(3)
         dx_sb[2] = slope[3][:]
         nc.vector.tensor_copy(dx_sb[2], dx_ps[2][:])
-        for kt in range(KT):
+        for kt in (2, 3):
+            scatter(2, kt, False)
+            scatter(1, kt, True)
+        for kt in (0, 1):
             scatter(2, kt, False)
         dx_sb[3] = work.tile([P, KT, C], F32, name="dx_sb", align_bytes=64)[:]
         nc.vector.tensor_copy(dx_sb[3][:, 0:2, :], dx_ps[3][0][:])

@@ -21,6 +21,7 @@ P = 128
 PASSES = N // 512
 KT = K // P
 LIST_COLS = C // 16
+ON_GPSIMD = 2
 
 
 def tile_moe_bdx_glu_silu_kernel(
@@ -93,10 +94,9 @@ def tile_moe_bdx_glu_silu_kernel(
         load_words("w2", w2_w, w2_words, 2, 3)
         load_words("w2", w2_w, w2_words, 3, 4)
         load_words("w3", w3_w, w3_words, 0, 1)
-        load_saved("a3", a3_t, a3, 2, 3)
+        load_saved("a3", a3_t, a3, 2, 4)
         load_words("w1", w1_w, w1_words, 1, 4)
         load_words("w3", w3_w, w3_words, 1, 4)
-        load_saved("a3", a3_t, a3, 3, 4)
 
         g_w, g_s = {}, {}
 
@@ -125,10 +125,11 @@ def tile_moe_bdx_glu_silu_kernel(
             nc.scalar.activation(silu_neg[e][:], a1_t[e], ACT.Silu, scale=-1.0)
             tanh_half[e] = work.tile([P, 4, C], F32, name="tanh_half", align_bytes=64)
             nc.scalar.activation(tanh_half[e][:], a1_t[e], ACT.Tanh, scale=0.5)
-            rest = work.tile([P, 4, C], F32, name="rest", align_bytes=64)
-            nc.gpsimd.tensor_scalar(rest[:], silu_neg[e][:], -1.0, 1.0, ALU.mult, ALU.add)
             slope[e] = work.tile([P, 4, C], F32, name="slope", align_bytes=64)
-            nc.gpsimd.tensor_tensor(slope[e][:], rest[:], a3_t[e], ALU.mult)
+            if e < ON_GPSIMD:
+                rest = work.tile([P, 4, C], F32, name="rest", align_bytes=64)
+                nc.gpsimd.tensor_scalar(rest[:], silu_neg[e][:], -1.0, 1.0, ALU.mult, ALU.add)
+                nc.gpsimd.tensor_tensor(slope[e][:], rest[:], a3_t[e], ALU.mult)
 
         def first_product(e):
             dh_ps = ps_dh.tile([P, H], F32, name="dh_ps")
@@ -148,9 +149,15 @@ def tile_moe_bdx_glu_silu_kernel(
             sig_dh = work.tile([P, 4, C], F32, name="sig_dh", align_bytes=64)
             nc.vector.scalar_tensor_tensor(sig_dh[:], tanh_half[e][:], 1.0, dh[e][:], ALU.add, ALU.mult)
             da = work.tile([P, 2, C, 4], BF16, name="da", align_bytes=64)
-            for which, factor in enumerate((a1_t[e], slope[e][:])):
-                nc.vector.tensor_tensor(
-                    da[:, which].rearrange("p (c i) t -> p c t i", i=2), by_pairs(sig_dh[:]), by_pairs(factor), ALU.mult
+            if e >= ON_GPSIMD:
+                nc.vector.scalar_tensor_tensor(slope[e][:], silu_neg[e][:], 1.0, a3_t[e], ALU.subtract, ALU.mult)
+            da_pairs = da[:].rearrange("p w (c i) t -> p w c t i", i=2)
+            nc.vector.tensor_tensor(da_pairs[:, 0], by_pairs(sig_dh[:]), by_pairs(a1_t[e]), ALU.mult)
+            if e < ON_GPSIMD:
+                nc.vector.tensor_tensor(da_pairs[:, 1], by_pairs(sig_dh[:]), by_pairs(slope[e][:]), ALU.mult)
+            else:
+                nc.vector.scalar_tensor_tensor(
+                    da[:, 1], sig_dh[:].rearrange("p t c -> p c t"), -1.0, slope[e][:].rearrange("p t c -> p c t"), ALU.mult, ALU.mult
                 )
             codes = work.tile([P, 2 * C], U32, name="codes", align_bytes=64)
             da_s = work.tile([P, 2 * C], U8, name="da_s", align_bytes=64)
@@ -200,16 +207,13 @@ def tile_moe_bdx_glu_silu_kernel(
         multiply(2)
         dx_sb[1] = ring[:, 2 : KT + 2, :]
         nc.scalar.copy(dx_sb[1], dx_ps[1][:])
-        for kt in (0, 1):
+        for kt in range(KT):
             scatter(1, kt, True)
         multiply(3)
         dx_sb[2] = slope[3][:]
         nc.vector.tensor_copy(dx_sb[2], dx_ps[2][:])
-        for kt in (2, 3):
-            scatter(2, kt, False)
-            scatter(1, kt, True)
-        for kt in (0, 1):
-            scatter(2, kt, False)
+        for kt in (0, 2, 1, 3):
+            scatter(2, kt, kt >= 2)
         dx_sb[3] = work.tile([P, KT, C], F32, name="dx_sb", align_bytes=64)[:]
         nc.vector.tensor_copy(dx_sb[3][:, 0:2, :], dx_ps[3][0][:])
         nc.scalar.copy(dx_sb[3][:, 2:4, :], dx_ps[3][1][:])

@@ -21,7 +21,6 @@ P = 128
 PASSES = N // 512
 KT = K // P
 LIST_COLS = C // 16
-ON_GPSIMD = 2
 
 
 def tile_moe_bdx_glu_silu_kernel(
@@ -32,9 +31,10 @@ def tile_moe_bdx_glu_silu_kernel(
         keep = ctx.enter_context(tc.tile_pool(name="keep", bufs=1))
         work = ctx.enter_context(tc.tile_pool(name="work", bufs=E))
         reused = ctx.enter_context(tc.tile_pool(name="reused", bufs=1))
+        ps_early = ctx.enter_context(tc.psum_pool(name="ps_early", bufs=2))
         ps_dh = ctx.enter_context(tc.psum_pool(name="ps_dh", bufs=2))
-        ps_tr = ctx.enter_context(tc.psum_pool(name="ps_tr", bufs=3))
-        ps_dx = ctx.enter_context(tc.psum_pool(name="ps_dx", bufs=3))
+        ps_y = ctx.enter_context(tc.psum_pool(name="ps_y", bufs=2))
+        ps_dx = ctx.enter_context(tc.psum_pool(name="ps_dx", bufs=2))
 
         offsets = keep.tile([P, E * LIST_COLS], U16, name="offsets")
         dy_w = keep.tile([P, PASSES, T], I32, name="dy_w", align_bytes=64)
@@ -55,10 +55,7 @@ def tile_moe_bdx_glu_silu_kernel(
 
         def load_words(name, table, src, lo, hi):
             passes = src.shape[1]
-            if name == "w2" and lo == E - 1:
-                t = reused.tile([P, passes, 1024], U8, name="w2_last", align_bytes=64, offset=0)
-            else:
-                t = keep.tile([P, (hi - lo) * passes, 1024], U8, name="%s_%d" % (name, lo), align_bytes=64)
+            t = keep.tile([P, (hi - lo) * passes, 1024], U8, name="%s_%d" % (name, lo), align_bytes=64)
             rows = src.rearrange("e s p b -> p (e s) b").bitcast(I32)
             nc.sync.dma_start(out=t[:].bitcast(I32), in_=rows[:, lo * passes : hi * passes, :])
             for e in range(lo, hi):
@@ -70,30 +67,31 @@ def tile_moe_bdx_glu_silu_kernel(
             for e in range(lo, hi):
                 table[e] = t[:, :, (e - lo) * C : (e - lo + 1) * C]
 
+        w1_rows = w1_scales.rearrange("e s f n -> (e s) f n")
+        w3_rows = w3_scales.rearrange("e s f n -> (e s) f n")
         nc.gpsimd.memset(dy_s[:].rearrange("p a b -> p (a b)").bitcast(I32), 0)
         nc.gpsimd.memset(gate_rows[:], 0.0)
         make_identity(nc, ident[:])
         nc.sync.dma_start(offsets[:], offs)
         load_scales(nc.scalar, dy_s, dy_scales, 0, 2)
-        load_saved("a1", a1_t, a1, 0, 2)
+        load_saved("a1", a1_t, a1, 0, 1)
         load_scales(nc.sync, dy_s, dy_scales, 2, 4)
         nc.sync.dma_start(out=dy_w[:], in_=dy_words.rearrange("s p t d -> p s (t d)").bitcast(I32))
         load_words("w2", w2_w, w2_words, 0, 1)
-        load_scales(nc.sync, w2_s, w2_scales.rearrange("e s f n -> (e s) f n"))
         nc.sync.dma_start(out=gate_rows[0:E, :], in_=gate[0].rearrange("(e c) -> e c", e=E))
-        w1_rows = w1_scales.rearrange("e s f n -> (e s) f n")
-        w3_rows = w3_scales.rearrange("e s f n -> (e s) f n")
+        load_scales(nc.sync, w2_s, w2_scales.rearrange("e s f n -> (e s) f n"))
+        load_saved("a1", a1_t, a1, 1, 2)
+        load_scales(nc.sync, w3_s, w3_rows, 0, 1)
         load_saved("a3", a3_t, a3, 0, 2)
-        load_scales(nc.sync, w3_s, w3_rows, 0, 2)
-        load_words("w2", w2_w, w2_words, 1, 2)
-        load_scales(nc.sync, w3_s, w3_rows, 2, 4)
+        load_scales(nc.sync, w3_s, w3_rows, 1, 3)
         load_saved("a1", a1_t, a1, 2, 4)
+        load_scales(nc.sync, w3_s, w3_rows, 3, 4)
         load_scales(nc.sync, w1_s, w1_rows, 0, 2)
         load_words("w1", w1_w, w1_words, 0, 1)
+        load_words("w2", w2_w, w2_words, 1, 3)
         load_scales(nc.sync, w1_s, w1_rows, 2, 4)
-        load_words("w2", w2_w, w2_words, 2, 3)
-        load_words("w2", w2_w, w2_words, 3, 4)
         load_words("w3", w3_w, w3_words, 0, 1)
+        load_words("w2", w2_w, w2_words, 3, 4)
         load_saved("a3", a3_t, a3, 2, 4)
         load_words("w1", w1_w, w1_words, 1, 4)
         load_words("w3", w3_w, w3_words, 1, 4)
@@ -114,8 +112,8 @@ def tile_moe_bdx_glu_silu_kernel(
                     g_w[e, s] = words[:, (e - lo) * C : (e - lo + 1) * C]
 
         windows = [keep.tile([P, T], F32, name="window_%d" % kt, align_bytes=64) for kt in range(KT)]
-        ring = reused.tile([P, KT + 2, C], F32, name="ring", align_bytes=64, offset=0)
-        tanh_half, silu_neg, slope, dh, dx_ps, dx_sb = {}, {}, {}, {}, {}, {}
+        ring = keep.tile([P, KT + 2, C], F32, name="ring", align_bytes=64)
+        silu_neg, gated_sig, slope, y_ps, dx_ps, dx_sb = {}, {}, {}, {}, {}, {}
 
         def by_pairs(ap):
             return ap.rearrange("p t (c i) -> p c t i", i=2)
@@ -123,13 +121,27 @@ def tile_moe_bdx_glu_silu_kernel(
         def functions(e):
             silu_neg[e] = work.tile([P, 4, C], F32, name="silu_neg", align_bytes=64)
             nc.scalar.activation(silu_neg[e][:], a1_t[e], ACT.Silu, scale=-1.0)
-            tanh_half[e] = work.tile([P, 4, C], F32, name="tanh_half", align_bytes=64)
-            nc.scalar.activation(tanh_half[e][:], a1_t[e], ACT.Tanh, scale=0.5)
-            slope[e] = work.tile([P, 4, C], F32, name="slope", align_bytes=64)
-            if e < ON_GPSIMD:
+            turned = ps_early.tile([P, 4, P], F32, name="early")
+            for t in range(4):
+                nc.tensor.transpose(turned[:, t, :], a1_t[e][:, t, :], ident[:])
+            tanh_half = work.tile([P, 4, P], F32, name="tanh_half", align_bytes=64)
+            nc.scalar.activation(tanh_half[:], turned[:], ACT.Tanh, scale=0.5)
+            if e == 0:
+                gate_ps = ps_early.tile([P, 4, P], F32, name="early")
+                nc.tensor.transpose(gate_ps[:, 0, :], gate_rows[:], ident[:])
+                nc.scalar.activation(gate_half[:], gate_ps[:, 0, 0:E], ACT.Copy, scale=0.5)
+            gated_sig[e] = work.tile([P, 4, P], F32, name="gated_sig", align_bytes=64)
+            half = gate_half[:, e : e + 1]
+            nc.scalar.activation(gated_sig[e][:], tanh_half[:], ACT.Identity, scale=half, bias=half)
+
+        def make_slope(e):
+            if e < 2:
                 rest = work.tile([P, 4, C], F32, name="rest", align_bytes=64)
-                nc.gpsimd.tensor_scalar(rest[:], silu_neg[e][:], -1.0, 1.0, ALU.mult, ALU.add)
-                nc.gpsimd.tensor_tensor(slope[e][:], rest[:], a3_t[e], ALU.mult)
+            else:
+                rest = reused.tile([P, 4, C], F32, name="rest_%d" % e, align_bytes=64, offset=1024 * (e - 2))
+            nc.gpsimd.tensor_scalar(rest[:], silu_neg[e][:], -1.0, 1.0, ALU.mult, ALU.add)
+            slope[e] = work.tile([P, 4, C], F32, name="slope", align_bytes=64)
+            nc.gpsimd.tensor_tensor(slope[e][:], rest[:], a3_t[e], ALU.mult)
 
         def first_product(e):
             dh_ps = ps_dh.tile([P, H], F32, name="dh_ps")
@@ -139,35 +151,30 @@ def tile_moe_bdx_glu_silu_kernel(
                     rhs=w2_w[e][:, s, :].bitcast(FP4X4), rhs_scale=w2_s[:, e * PASSES + s, :],
                     start=(s == 0), stop=(s == PASSES - 1),
                 )
-            dh_sb = work.tile([P, 4, P], F32, name="dh_sb", align_bytes=64)
-            nc.scalar.activation(dh_sb[:], dh_ps[:].rearrange("c (p t) -> c t p", t=4), ACT.Copy, scale=gate_half[:, e : e + 1])
-            dh[e] = ps_tr.tile([P, 4, C], F32, name="dh")
+            y_sb = work.tile([P, 4, P], F32, name="y_sb", align_bytes=64)
+            nc.vector.tensor_tensor(y_sb[:], dh_ps[:].rearrange("c (p t) -> c t p", t=4), gated_sig[e][:], ALU.mult)
+            y_ps[e] = ps_y.tile([P, 4, C], F32, name="y_ps")
             for t in range(4):
-                nc.tensor.transpose(dh[e][:, t, :], dh_sb[:, t, :], ident[:])
+                nc.tensor.transpose(y_ps[e][:, t, :], y_sb[:, t, :], ident[:])
 
-        def multiply(e):
-            sig_dh = work.tile([P, 4, C], F32, name="sig_dh", align_bytes=64)
-            nc.vector.scalar_tensor_tensor(sig_dh[:], tanh_half[e][:], 1.0, dh[e][:], ALU.add, ALU.mult)
-            da = work.tile([P, 2, C, 4], BF16, name="da", align_bytes=64)
-            if e >= ON_GPSIMD:
-                nc.vector.scalar_tensor_tensor(slope[e][:], silu_neg[e][:], 1.0, a3_t[e], ALU.subtract, ALU.mult)
-            da_pairs = da[:].rearrange("p w (c i) t -> p w c t i", i=2)
-            nc.vector.tensor_tensor(da_pairs[:, 0], by_pairs(sig_dh[:]), by_pairs(a1_t[e]), ALU.mult)
-            if e < ON_GPSIMD:
-                nc.vector.tensor_tensor(da_pairs[:, 1], by_pairs(sig_dh[:]), by_pairs(slope[e][:]), ALU.mult)
+        def second_product(e):
+            if e < 2:
+                da = reused.tile([P, 2, C, 4], BF16, name="da_%d" % e, align_bytes=64, offset=2048 * e)
             else:
-                nc.vector.scalar_tensor_tensor(
-                    da[:, 1], sig_dh[:].rearrange("p t c -> p c t"), -1.0, slope[e][:].rearrange("p t c -> p c t"), ALU.mult, ALU.mult
+                da = work.tile([P, 2, C, 4], BF16, name="da", align_bytes=64)
+            for which, factor in enumerate((a1_t[e], slope[e][:])):
+                nc.vector.tensor_tensor(
+                    da[:, which].rearrange("p (c i) t -> p c t i", i=2), by_pairs(y_ps[e][:]), by_pairs(factor), ALU.mult
                 )
             codes = work.tile([P, 2 * C], U32, name="codes", align_bytes=64)
             da_s = work.tile([P, 2 * C], U8, name="da_s", align_bytes=64)
             nc.vector.quantize_mx(codes[:].bitcast(FP8X4), da_s[:], da[:].rearrange("p w j t -> p (w j t)"))
 
-            dx_ps[e] = [ps_dx.tile([P, 2, C], F32, name="dx_ps") for half in range(2)] if e == E - 1 else ps_dx.tile([P, KT, C], F32, name="dx_ps")
+            dx_ps[e] = ps_dx.tile([P, KT, C], F32, name="dx_ps") if e < 2 else ps_early.tile([P, KT, C], F32, name="early")
             for kt in range(KT):
                 for which, (words, plane) in enumerate(((w3_w, w3_s), (w1_w, w1_s))):
                     nc.tensor.matmul_mx(
-                        dx_ps[e][kt // 2][:, kt % 2, :] if e == E - 1 else dx_ps[e][:, kt, :],
+                        dx_ps[e][:, kt, :],
                         lhsT=words[e][:, 0, kt * 256 : (kt + 1) * 256].bitcast(FP4X4),
                         lhsT_scale=plane[:, e, kt * P : (kt + 1) * P],
                         rhs=codes[:, which * C : (which + 1) * C].bitcast(FP8X4),
@@ -186,36 +193,39 @@ def tile_moe_bdx_glu_silu_kernel(
 
         gather(0, 1, "outer")
         gather(1, 3, "inner")
-        gate_ps = ps_tr.tile([P, 4, C], F32, name="dh")
-        nc.tensor.transpose(gate_ps[:, 0, :], gate_rows[:], ident[:])
-        nc.scalar.activation(gate_half[:], gate_ps[:, 0, 0:E], ACT.Copy, scale=0.5)
         functions(0)
+        make_slope(0)
         first_product(0)
         gather(3, 4, "outer")
         functions(1)
+        make_slope(1)
         first_product(1)
-        multiply(0)
-        for e in range(2, E):
-            functions(e)
-        for e in range(2, E):
-            first_product(e)
-        multiply(1)
+        second_product(0)
         dx_sb[0] = ring[:, 0:KT, :]
         nc.scalar.copy(dx_sb[0], dx_ps[0][:])
+        for e in range(2, E):
+            functions(e)
+        make_slope(2)
+        first_product(2)
+        second_product(1)
+        make_slope(3)
+        first_product(3)
         for kt in reversed(range(KT)):
             scatter(0, kt, True)
-        multiply(2)
+        second_product(2)
         dx_sb[1] = ring[:, 2 : KT + 2, :]
         nc.scalar.copy(dx_sb[1], dx_ps[1][:])
-        for kt in range(KT):
+        for kt in (0, 1):
             scatter(1, kt, True)
-        multiply(3)
+        second_product(3)
         dx_sb[2] = slope[3][:]
         nc.vector.tensor_copy(dx_sb[2], dx_ps[2][:])
-        for kt in (0, 2, 1, 3):
-            scatter(2, kt, kt >= 2)
+        for kt in (2, 3):
+            scatter(2, kt, False)
+            scatter(1, kt, True)
         dx_sb[3] = work.tile([P, KT, C], F32, name="dx_sb", align_bytes=64)[:]
-        nc.vector.tensor_copy(dx_sb[3][:, 0:2, :], dx_ps[3][0][:])
-        nc.scalar.copy(dx_sb[3][:, 2:4, :], dx_ps[3][1][:])
+        nc.vector.tensor_copy(dx_sb[3], dx_ps[3][:])
+        for kt in (0, 1):
+            scatter(2, kt, kt == 1)
         for kt in (0, 2, 1, 3):
             scatter(3, kt, kt >= 2)

@@ -67,8 +67,6 @@ def tile_moe_bdx_glu_silu_kernel(
             for e in range(lo, hi):
                 table[e] = t[:, :, (e - lo) * C : (e - lo + 1) * C]
 
-        w1_rows = w1_scales.rearrange("e s f n -> (e s) f n")
-        w3_rows = w3_scales.rearrange("e s f n -> (e s) f n")
         nc.gpsimd.memset(dy_s[:].rearrange("p a b -> p (a b)").bitcast(I32), 0)
         nc.gpsimd.memset(gate_rows[:], 0.0)
         make_identity(nc, ident[:])
@@ -79,17 +77,17 @@ def tile_moe_bdx_glu_silu_kernel(
         nc.sync.dma_start(out=dy_w[:], in_=dy_words.rearrange("s p t d -> p s (t d)").bitcast(I32))
         load_words("w2", w2_w, w2_words, 0, 1)
         nc.sync.dma_start(out=gate_rows[0:E, :], in_=gate[0].rearrange("(e c) -> e c", e=E))
-        load_scales(nc.sync, w2_s, w2_scales.rearrange("e s f n -> (e s) f n"))
+        load_scales(nc.sync, w2_s, w2_scales.rearrange("e s f n -> (e s) f n"), 0, 4)
         load_saved("a1", a1_t, a1, 1, 2)
-        load_scales(nc.sync, w3_s, w3_rows, 0, 1)
         load_saved("a3", a3_t, a3, 0, 2)
-        load_scales(nc.sync, w3_s, w3_rows, 1, 3)
+        load_words("w2", w2_w, w2_words, 1, 2)
         load_saved("a1", a1_t, a1, 2, 4)
-        load_scales(nc.sync, w3_s, w3_rows, 3, 4)
-        load_scales(nc.sync, w1_s, w1_rows, 0, 2)
+        load_scales(nc.sync, w3_s, w3_scales.rearrange("e s f n -> (e s) f n"), 0, 2)
+        load_words("w2", w2_w, w2_words, 2, 3)
+        load_scales(nc.sync, w3_s, w3_scales.rearrange("e s f n -> (e s) f n"), 2, 4)
+        load_scales(nc.sync, w1_s, w1_scales.rearrange("e s f n -> (e s) f n"), 0, 2)
         load_words("w1", w1_w, w1_words, 0, 1)
-        load_words("w2", w2_w, w2_words, 1, 3)
-        load_scales(nc.sync, w1_s, w1_rows, 2, 4)
+        load_scales(nc.sync, w1_s, w1_scales.rearrange("e s f n -> (e s) f n"), 2, 4)
         load_words("w3", w3_w, w3_words, 0, 1)
         load_words("w2", w2_w, w2_words, 3, 4)
         load_saved("a3", a3_t, a3, 2, 4)
@@ -134,14 +132,22 @@ def tile_moe_bdx_glu_silu_kernel(
             half = gate_half[:, e : e + 1]
             nc.scalar.activation(gated_sig[e][:], tanh_half[:], ACT.Identity, scale=half, bias=half)
 
-        def make_slope(e):
+        rests = {}
+
+        def make_rest(e):
             if e < 2:
                 rest = work.tile([P, 4, C], F32, name="rest", align_bytes=64)
             else:
-                rest = reused.tile([P, 4, C], F32, name="rest_%d" % e, align_bytes=64, offset=1024 * (e - 2))
+                rest = reused.tile([P, 4, C], F32, name="rest_%d" % e, align_bytes=64, offset=2048 * (e - 2))
             nc.gpsimd.tensor_scalar(rest[:], silu_neg[e][:], -1.0, 1.0, ALU.mult, ALU.add)
-            slope[e] = work.tile([P, 4, C], F32, name="slope", align_bytes=64)
-            nc.gpsimd.tensor_tensor(slope[e][:], rest[:], a3_t[e], ALU.mult)
+            rests[e] = rest
+
+        def make_slope(e):
+            if e == 2:
+                slope[e] = reused.tile([P, 4, C], F32, name="slope_2", align_bytes=64, offset=4096)
+            else:
+                slope[e] = work.tile([P, 4, C], F32, name="slope", align_bytes=64)
+            nc.gpsimd.tensor_tensor(slope[e][:], rests[e][:], a3_t[e], ALU.mult)
 
         def first_product(e):
             dh_ps = ps_dh.tile([P, H], F32, name="dh_ps")
@@ -151,7 +157,10 @@ def tile_moe_bdx_glu_silu_kernel(
                     rhs=w2_w[e][:, s, :].bitcast(FP4X4), rhs_scale=w2_s[:, e * PASSES + s, :],
                     start=(s == 0), stop=(s == PASSES - 1),
                 )
-            y_sb = work.tile([P, 4, P], F32, name="y_sb", align_bytes=64)
+            if e == 2:
+                y_sb = reused.tile([P, 4, P], F32, name="y_sb_2", align_bytes=64, offset=6144)
+            else:
+                y_sb = work.tile([P, 4, P], F32, name="y_sb", align_bytes=64)
             nc.vector.tensor_tensor(y_sb[:], dh_ps[:].rearrange("c (p t) -> c t p", t=4), gated_sig[e][:], ALU.mult)
             y_ps[e] = ps_y.tile([P, 4, C], F32, name="y_ps")
             for t in range(4):
@@ -159,22 +168,30 @@ def tile_moe_bdx_glu_silu_kernel(
 
         def second_product(e):
             if e < 2:
-                da = reused.tile([P, 2, C, 4], BF16, name="da_%d" % e, align_bytes=64, offset=2048 * e)
+                da = reused.tile([P, 2, C, 4], BF16, name="da_%d" % e, align_bytes=64, offset=(1024, 4096)[e])
             else:
                 da = work.tile([P, 2, C, 4], BF16, name="da", align_bytes=64)
             for which, factor in enumerate((a1_t[e], slope[e][:])):
                 nc.vector.tensor_tensor(
                     da[:, which].rearrange("p (c i) t -> p c t i", i=2), by_pairs(y_ps[e][:]), by_pairs(factor), ALU.mult
                 )
-            codes = work.tile([P, 2 * C], U32, name="codes", align_bytes=64)
+            if e == 0:
+                codes = reused.tile([P, 2 * C], U32, name="codes_0", align_bytes=64, offset=6144)
+            else:
+                codes = work.tile([P, 2 * C], U32, name="codes", align_bytes=64)
             da_s = work.tile([P, 2 * C], U8, name="da_s", align_bytes=64)
-            nc.vector.quantize_mx(codes[:].bitcast(FP8X4), da_s[:], da[:].rearrange("p w j t -> p (w j t)"))
+            for which in range(2):
+                cols = slice(which * C, (which + 1) * C)
+                nc.vector.quantize_mx(codes[:, cols].bitcast(FP8X4), da_s[:, cols], da[:, which].rearrange("p j t -> p (j t)"))
 
-            dx_ps[e] = ps_dx.tile([P, KT, C], F32, name="dx_ps") if e < 2 else ps_early.tile([P, KT, C], F32, name="early")
+            if e == E - 1:
+                dx_ps[e] = [ps_early.tile([P, 2, C], F32, name="early"), ps_dx.tile([P, 2, C], F32, name="dx_ps")]
+            else:
+                dx_ps[e] = ps_dx.tile([P, KT, C], F32, name="dx_ps") if e < 2 else ps_early.tile([P, KT, C], F32, name="early")
             for kt in range(KT):
                 for which, (words, plane) in enumerate(((w3_w, w3_s), (w1_w, w1_s))):
                     nc.tensor.matmul_mx(
-                        dx_ps[e][:, kt, :],
+                        dx_ps[e][kt // 2][:, kt % 2, :] if e == E - 1 else dx_ps[e][:, kt, :],
                         lhsT=words[e][:, 0, kt * 256 : (kt + 1) * 256].bitcast(FP4X4),
                         lhsT_scale=plane[:, e, kt * P : (kt + 1) * P],
                         rhs=codes[:, which * C : (which + 1) * C].bitcast(FP8X4),
@@ -189,15 +206,18 @@ def tile_moe_bdx_glu_silu_kernel(
             else:
                 nc.vector.tensor_copy(windows[kt][:].indirect(picks), dx_sb[e][:, kt, :])
             if e == E - 1:
-                nc.sync.dma_start(out=out[kt * P : (kt + 1) * P, :], in_=windows[kt][:])
+                queue = nc.scalar if kt == 3 else nc.sync
+                queue.dma_start(out=out[kt * P : (kt + 1) * P, :], in_=windows[kt][:])
 
         gather(0, 1, "outer")
         gather(1, 3, "inner")
         functions(0)
+        make_rest(0)
         make_slope(0)
         first_product(0)
         gather(3, 4, "outer")
         functions(1)
+        make_rest(1)
         make_slope(1)
         first_product(1)
         second_product(0)
@@ -205,9 +225,11 @@ def tile_moe_bdx_glu_silu_kernel(
         nc.scalar.copy(dx_sb[0], dx_ps[0][:])
         for e in range(2, E):
             functions(e)
-        make_slope(2)
+        make_rest(2)
+        make_rest(3)
         first_product(2)
         second_product(1)
+        make_slope(2)
         make_slope(3)
         first_product(3)
         for kt in reversed(range(KT)):
@@ -224,8 +246,9 @@ def tile_moe_bdx_glu_silu_kernel(
             scatter(2, kt, False)
             scatter(1, kt, True)
         dx_sb[3] = work.tile([P, KT, C], F32, name="dx_sb", align_bytes=64)[:]
-        nc.vector.tensor_copy(dx_sb[3], dx_ps[3][:])
         for kt in (0, 1):
             scatter(2, kt, kt == 1)
+        nc.vector.tensor_copy(dx_sb[3][:, 0:2, :], dx_ps[3][0][:])
+        nc.scalar.copy(dx_sb[3][:, 2:4, :], dx_ps[3][1][:])
         for kt in (0, 2, 1, 3):
             scatter(3, kt, kt >= 2)

@@ -79,8 +79,8 @@ def tile_moe_bdx_glu_silu_kernel(
         nc.sync.dma_start(out=gate_rows[0:E, :], in_=gate[0].rearrange("(e c) -> e c", e=E))
         load_scales(nc.sync, w2_s, w2_scales.rearrange("e s f n -> (e s) f n"), 0, 4)
         load_saved("a1", a1_t, a1, 1, 2)
-        load_saved("a3", a3_t, a3, 0, 2)
         load_words("w2", w2_w, w2_words, 1, 2)
+        load_saved("a3", a3_t, a3, 0, 2)
         load_saved("a1", a1_t, a1, 2, 4)
         load_scales(nc.sync, w3_s, w3_scales.rearrange("e s f n -> (e s) f n"), 0, 2)
         load_words("w2", w2_w, w2_words, 2, 3)
@@ -219,12 +219,12 @@ def tile_moe_bdx_glu_silu_kernel(
         functions(1)
         make_rest(1)
         make_slope(1)
+        for e in range(2, E):
+            functions(e)
         first_product(1)
         second_product(0)
         dx_sb[0] = ring[:, 0:KT, :]
         nc.scalar.copy(dx_sb[0], dx_ps[0][:])
-        for e in range(2, E):
-            functions(e)
         make_rest(2)
         make_rest(3)
         first_product(2)

@@ -91,8 +91,10 @@ def tile_moe_bdx_glu_silu_kernel(
         load_words("w3", w3_w, w3_words, 0, 1)
         load_words("w2", w2_w, w2_words, 3, 4)
         load_saved("a3", a3_t, a3, 2, 4)
-        load_words("w1", w1_w, w1_words, 1, 4)
-        load_words("w3", w3_w, w3_words, 1, 4)
+        load_words("w1", w1_w, w1_words, 1, 2)
+        load_words("w3", w3_w, w3_words, 1, 2)
+        load_words("w1", w1_w, w1_words, 2, 4)
+        load_words("w3", w3_w, w3_words, 2, 4)
 
         g_w, g_s = {}, {}
 

@@ -112,7 +112,6 @@ def tile_moe_bdx_glu_silu_kernel(
                     g_w[e, s] = words[:, (e - lo) * C : (e - lo + 1) * C]
 
         windows = [keep.tile([P, T], F32, name="window_%d" % kt, align_bytes=64) for kt in range(KT)]
-        ring = keep.tile([P, KT + 2, C], F32, name="ring", align_bytes=64)
         silu_neg, gated_sig, slope, y_ps, dx_ps, dx_sb = {}, {}, {}, {}, {}, {}
 
         def by_pairs(ap):
@@ -168,11 +167,13 @@ def tile_moe_bdx_glu_silu_kernel(
             for t in range(4):
                 nc.tensor.transpose(y_ps[e][:, t, :], y_sb[:, t, :], ident[:])
 
+        dx_whole = {}
+
         def second_product(e):
             if e < 2:
                 da = reused.tile([P, 2, C, 4], BF16, name="da_%d" % e, align_bytes=64, offset=(1024, 4096)[e])
             else:
-                da = work.tile([P, 2, C, 4], BF16, name="da", align_bytes=64)
+                da = reused.tile([P, 2, C, 4], BF16, name="da_%d" % e, align_bytes=64, offset=8192 + 2048 * (e - 2))
             for which, factor in enumerate((a1_t[e], slope[e][:])):
                 nc.vector.tensor_tensor(
                     da[:, which].rearrange("p (c i) t -> p c t i", i=2), by_pairs(y_ps[e][:]), by_pairs(factor), ALU.mult
@@ -186,14 +187,17 @@ def tile_moe_bdx_glu_silu_kernel(
                 cols = slice(which * C, (which + 1) * C)
                 nc.vector.quantize_mx(codes[:, cols].bitcast(FP8X4), da_s[:, cols], da[:, which].rearrange("p j t -> p (j t)"))
 
-            if e == E - 1:
-                dx_ps[e] = [ps_early.tile([P, 2, C], F32, name="early"), ps_dx.tile([P, 2, C], F32, name="dx_ps")]
+            if e == 2:
+                dx_whole[e] = ps_early.tile([P, KT, C], F32, name="early")
+                dx_ps[e] = [dx_whole[e][:, 0:2, :], dx_whole[e][:, 2:4, :]]
+            elif e == 3:
+                dx_ps[e] = [ps_early.tile([P, 2, C], F32, name="early")[:], ps_dx.tile([P, 2, C], F32, name="dx_ps")[:]]
             else:
-                dx_ps[e] = ps_dx.tile([P, KT, C], F32, name="dx_ps") if e < 2 else ps_early.tile([P, KT, C], F32, name="early")
+                dx_ps[e] = [ps_dx.tile([P, 2, C], F32, name="dx_ps")[:] for h in range(2)]
             for kt in range(KT):
                 for which, (words, plane) in enumerate(((w3_w, w3_s), (w1_w, w1_s))):
                     nc.tensor.matmul_mx(
-                        dx_ps[e][kt // 2][:, kt % 2, :] if e == E - 1 else dx_ps[e][:, kt, :],
+                        dx_ps[e][kt // 2][:, kt % 2, :],
                         lhsT=words[e][:, 0, kt * 256 : (kt + 1) * 256].bitcast(FP4X4),
                         lhsT_scale=plane[:, e, kt * P : (kt + 1) * P],
                         rhs=codes[:, which * C : (which + 1) * C].bitcast(FP8X4),
@@ -201,12 +205,23 @@ def tile_moe_bdx_glu_silu_kernel(
                         start=(which == 0), stop=(which == 1),
                     )
 
+        def copy_out(e, h, on_scalar):
+            if (e, h) == (1, 1):
+                t = reused.tile([P, 2, C], F32, name="dx_sb_late", align_bytes=64, offset=10240)
+            else:
+                t = keep.tile([P, 2, C], F32, name="dx_sb_%d_%d" % (e, h), align_bytes=64)
+            dx_sb[e, h] = t[:]
+            if on_scalar:
+                nc.scalar.copy(t[:], dx_ps[e][h])
+            else:
+                nc.vector.tensor_copy(t[:], dx_ps[e][h])
+
         def scatter(e, kt, on_scalar):
             picks = offsets[:, e * LIST_COLS : (e + 1) * LIST_COLS]
             if on_scalar:
-                nc.scalar.activation(windows[kt][:].indirect(picks), dx_sb[e][:, kt, :], ACT.Copy)
+                nc.scalar.activation(windows[kt][:].indirect(picks), dx_sb[e, kt // 2][:, kt % 2, :], ACT.Copy)
             else:
-                nc.vector.tensor_copy(windows[kt][:].indirect(picks), dx_sb[e][:, kt, :])
+                nc.vector.tensor_copy(windows[kt][:].indirect(picks), dx_sb[e, kt // 2][:, kt % 2, :])
             if e == E - 1:
                 queue = nc.scalar if kt == 3 else nc.sync
                 queue.dma_start(out=out[kt * P : (kt + 1) * P, :], in_=windows[kt][:])
@@ -225,8 +240,10 @@ def tile_moe_bdx_glu_silu_kernel(
             functions(e)
         first_product(1)
         second_product(0)
-        dx_sb[0] = ring[:, 0:KT, :]
-        nc.scalar.copy(dx_sb[0], dx_ps[0][:])
+        for h in range(2):
+            copy_out(0, h, True)
+            scatter(0, 2 * h, True)
+            scatter(0, 2 * h + 1, True)
         make_rest(2)
         make_rest(3)
         first_product(2)
@@ -234,23 +251,20 @@ def tile_moe_bdx_glu_silu_kernel(
         make_slope(2)
         make_slope(3)
         first_product(3)
-        for kt in reversed(range(KT)):
-            scatter(0, kt, True)
+        copy_out(1, 0, True)
+        for kt in (0, 1):
+            scatter(1, kt, True)
         second_product(2)
-        dx_sb[1] = ring[:, 2 : KT + 2, :]
-        nc.scalar.copy(dx_sb[1], dx_ps[1][:])
-        for kt in (0, 1):
-            scatter(1, kt, True)
         second_product(3)
-        dx_sb[2] = slope[3][:]
-        nc.vector.tensor_copy(dx_sb[2], dx_ps[2][:])
+        copy_out(1, 1, False)
         for kt in (2, 3):
-            scatter(2, kt, False)
-            scatter(1, kt, True)
-        dx_sb[3] = work.tile([P, KT, C], F32, name="dx_sb", align_bytes=64)[:]
-        for kt in (0, 1):
-            scatter(2, kt, kt == 1)
-        nc.vector.tensor_copy(dx_sb[3][:, 0:2, :], dx_ps[3][0][:])
-        nc.scalar.copy(dx_sb[3][:, 2:4, :], dx_ps[3][1][:])
-        for kt in (0, 2, 1, 3):
-            scatter(3, kt, kt >= 2)
+            scatter(1, kt, False)
+        dx_2 = keep.tile([P, KT, C], F32, name="dx_sb_2", align_bytes=64)
+        nc.scalar.copy(dx_2[:], dx_whole[2][:])
+        dx_sb[2, 0], dx_sb[2, 1] = dx_2[:, 0:2, :], dx_2[:, 2:4, :]
+        for kt in range(KT):
+            scatter(2, kt, True)
+        copy_out(3, 0, False)
+        copy_out(3, 1, True)
+        for kt in range(KT):
+            scatter(3, kt, kt == 3)

@@ -37,7 +37,7 @@ def tile_moe_bdx_glu_silu_kernel(
         ps_dx = ctx.enter_context(tc.psum_pool(name="ps_dx", bufs=2))
 
         offsets = keep.tile([P, E * LIST_COLS], U16, name="offsets")
-        dy_w = keep.tile([P, PASSES, T], I32, name="dy_w", align_bytes=64)
+        dy_w = reused.tile([P, PASSES, T], I32, name="dy_w", align_bytes=64, offset=12288)
         dy_s = keep.tile([P, PASSES, T], U8, name="dy_s", align_bytes=64)
         w2_s = keep.tile([P, E * PASSES, H], U8, name="w2_s", align_bytes=64)
         w1_s = keep.tile([P, E, K], U8, name="w1_s", align_bytes=64)
@@ -136,16 +136,18 @@ def tile_moe_bdx_glu_silu_kernel(
         rests = {}
 
         def make_rest(e):
-            if e < 2:
+            if e == 0:
                 rest = work.tile([P, 4, C], F32, name="rest", align_bytes=64)
+                nc.scalar.activation(rest[:], silu_neg[e][:], ACT.Copy, scale=-1.0, bias=1.0)
             else:
-                rest = reused.tile([P, 4, C], F32, name="rest_%d" % e, align_bytes=64, offset=2048 * (e - 2))
-            nc.gpsimd.tensor_scalar(rest[:], silu_neg[e][:], -1.0, 1.0, ALU.mult, ALU.add)
+                at = (16384, 0, 2048)[e - 1]
+                rest = reused.tile([P, 4, C], F32, name="rest_%d" % e, align_bytes=64, offset=at)
+                nc.gpsimd.tensor_scalar(rest[:], silu_neg[e][:], -1.0, 1.0, ALU.mult, ALU.add)
             rests[e] = rest
 
         def make_slope(e):
-            if e == 2:
-                slope[e] = reused.tile([P, 4, C], F32, name="slope_2", align_bytes=64, offset=4096)
+            if e % 2 == 0:
+                slope[e] = reused.tile([P, 4, C], F32, name="slope_%d" % e, align_bytes=64, offset=(12288, 4096)[e // 2])
             else:
                 slope[e] = work.tile([P, 4, C], F32, name="slope", align_bytes=64)
             nc.gpsimd.tensor_tensor(slope[e][:], rests[e][:], a3_t[e], ALU.mult)
@@ -183,9 +185,12 @@ def tile_moe_bdx_glu_silu_kernel(
             else:
                 codes = work.tile([P, 2 * C], U32, name="codes", align_bytes=64)
             da_s = work.tile([P, 2 * C], U8, name="da_s", align_bytes=64)
-            for which in range(2):
-                cols = slice(which * C, (which + 1) * C)
-                nc.vector.quantize_mx(codes[:, cols].bitcast(FP8X4), da_s[:, cols], da[:, which].rearrange("p j t -> p (j t)"))
+            if e == 0:
+                nc.vector.quantize_mx(codes[:].bitcast(FP8X4), da_s[:], da[:].rearrange("p w j t -> p (w j t)"))
+            else:
+                for which in range(2):
+                    cols = slice(which * C, (which + 1) * C)
+                    nc.vector.quantize_mx(codes[:, cols].bitcast(FP8X4), da_s[:, cols], da[:, which].rearrange("p j t -> p (j t)"))
 
             if e == 2:
                 dx_whole[e] = ps_early.tile([P, KT, C], F32, name="early")
@@ -230,9 +235,9 @@ def tile_moe_bdx_glu_silu_kernel(
         gather(1, 3, "inner")
         functions(0)
         make_rest(0)
-        make_slope(0)
         first_product(0)
         gather(3, 4, "outer")
+        make_slope(0)
         functions(1)
         make_rest(1)
         make_slope(1)

@@ -21,6 +21,7 @@ P = 128
 PASSES = N // 512
 KT = K // P
 LIST_COLS = C // 16
+KB = 1024
 
 
 def tile_moe_bdx_glu_silu_kernel(
@@ -29,22 +30,34 @@ def tile_moe_bdx_glu_silu_kernel(
     nc = tc.nc
     with ExitStack() as ctx:
         keep = ctx.enter_context(tc.tile_pool(name="keep", bufs=1))
-        work = ctx.enter_context(tc.tile_pool(name="work", bufs=E))
         reused = ctx.enter_context(tc.tile_pool(name="reused", bufs=1))
-        ps_early = ctx.enter_context(tc.psum_pool(name="ps_early", bufs=2))
-        ps_dh = ctx.enter_context(tc.psum_pool(name="ps_dh", bufs=2))
-        ps_y = ctx.enter_context(tc.psum_pool(name="ps_y", bufs=2))
-        ps_dx = ctx.enter_context(tc.psum_pool(name="ps_dx", bufs=2))
+        by_vector = ctx.enter_context(tc.tile_pool(name="by_vector", bufs=28))
+        by_scalar = ctx.enter_context(tc.tile_pool(name="by_scalar", bufs=24))
+        banks = ctx.enter_context(tc.psum_pool(name="banks", bufs=8))
+
+        def v_tile(shape, dtype):
+            return by_vector.tile(shape, dtype, name="v", align_bytes=64)
+
+        def s_tile(shape, dtype):
+            return by_scalar.tile(shape, dtype, name="s", align_bytes=64)
+
+        def bank(shape):
+            return banks.tile(shape, F32, name="bank")
+
+        def place(name, shape, dtype, at=None):
+            if at is None:
+                return keep.tile(shape, dtype, name=name, align_bytes=64)
+            return reused.tile(shape, dtype, name=name, align_bytes=64, offset=at)
 
         offsets = keep.tile([P, E * LIST_COLS], U16, name="offsets")
-        dy_w = reused.tile([P, PASSES, T], I32, name="dy_w", align_bytes=64, offset=12288)
-        dy_s = keep.tile([P, PASSES, T], U8, name="dy_s", align_bytes=64)
-        w2_s = keep.tile([P, E * PASSES, H], U8, name="w2_s", align_bytes=64)
-        w1_s = keep.tile([P, E, K], U8, name="w1_s", align_bytes=64)
-        w3_s = keep.tile([P, E, K], U8, name="w3_s", align_bytes=64)
-        ident = keep.tile([P, P], F32, name="ident", align_bytes=64)
-        gate_rows = keep.tile([P, C], F32, name="gate_rows", align_bytes=64)
-        gate_half = keep.tile([P, E], F32, name="gate_half")
+        dy_w = place("dy_w", [P, PASSES, T], I32)
+        dy_s = place("dy_s", [P, PASSES, T], U8)
+        dy_s_rows = place("dy_s_rows", [4, PASSES, 4, T], U8)
+        w2_s = place("w2_s", [P, E * PASSES, H], U8)
+        w1_s = place("w1_s", [P, E, K], U8)
+        w3_s = place("w3_s", [P, E, K], U8)
+        ident = place("ident", [P, P], F32)
+        gate_rows = place("gate_rows", [P, C], F32)
 
         def load_scales(queue, plane, rows, lo=0, hi=4):
             by_row = rows.rearrange("a (q r) n -> r q a n", r=4)
@@ -55,40 +68,42 @@ def tile_moe_bdx_glu_silu_kernel(
 
         def load_words(name, table, src, lo, hi):
             passes = src.shape[1]
-            t = keep.tile([P, (hi - lo) * passes, 1024], U8, name="%s_%d" % (name, lo), align_bytes=64)
+            t = place("%s_%d" % (name, lo), [P, (hi - lo) * passes, 1024], U8)
             rows = src.rearrange("e s p b -> p (e s) b").bitcast(I32)
             nc.sync.dma_start(out=t[:].bitcast(I32), in_=rows[:, lo * passes : hi * passes, :])
             for e in range(lo, hi):
                 table[e] = t[:, (e - lo) * passes : (e - lo + 1) * passes, :]
 
         def load_saved(name, table, src, lo, hi):
-            t = keep.tile([P, 4, (hi - lo) * C], F32, name="%s_%d" % (name, lo), align_bytes=64)
+            t = place("%s_%d" % (name, lo), [P, 4, (hi - lo) * C], F32)
             nc.sync.dma_start(out=t[:], in_=src.rearrange("(p t) j -> p t j", t=4)[:, :, lo * C : hi * C])
             for e in range(lo, hi):
                 table[e] = t[:, :, (e - lo) * C : (e - lo + 1) * C]
+
+        w2_rows = w2_scales.rearrange("e s f n -> (e s) f n")
+        w1_rows = w1_scales.rearrange("e s f n -> (e s) f n")
+        w3_rows = w3_scales.rearrange("e s f n -> (e s) f n")
 
         nc.gpsimd.memset(dy_s[:].rearrange("p a b -> p (a b)").bitcast(I32), 0)
         nc.gpsimd.memset(gate_rows[:], 0.0)
         make_identity(nc, ident[:])
         nc.sync.dma_start(offsets[:], offs)
-        load_scales(nc.scalar, dy_s, dy_scales, 0, 2)
+        nc.scalar.dma_start(out=dy_s_rows[:].rearrange("r s q n -> r (s q) n").bitcast(I32), in_=dy_scales.rearrange("s (q r) n -> r (s q) n", r=4).bitcast(I32))
         load_saved("a1", a1_t, a1, 0, 1)
-        load_scales(nc.sync, dy_s, dy_scales, 2, 4)
+        nc.sync.dma_start(out=gate_rows[0:E, :], in_=gate[0].rearrange("(e c) -> e c", e=E))
+        load_saved("a1", a1_t, a1, 1, 2)
         nc.sync.dma_start(out=dy_w[:], in_=dy_words.rearrange("s p t d -> p s (t d)").bitcast(I32))
         load_words("w2", w2_w, w2_words, 0, 1)
-        nc.sync.dma_start(out=gate_rows[0:E, :], in_=gate[0].rearrange("(e c) -> e c", e=E))
-        load_scales(nc.sync, w2_s, w2_scales.rearrange("e s f n -> (e s) f n"), 0, 4)
-        load_saved("a1", a1_t, a1, 1, 2)
-        load_words("w2", w2_w, w2_words, 1, 2)
-        load_saved("a3", a3_t, a3, 0, 2)
+        load_scales(nc.sync, w2_s, w2_rows, 0, 4)
         load_saved("a1", a1_t, a1, 2, 4)
-        load_scales(nc.sync, w3_s, w3_scales.rearrange("e s f n -> (e s) f n"), 0, 2)
+        load_saved("a3", a3_t, a3, 0, 1)
+        load_words("w2", w2_w, w2_words, 1, 2)
+        load_saved("a3", a3_t, a3, 1, 2)
+        load_scales(nc.sync, w3_s, w3_rows, 0, 4)
         load_words("w2", w2_w, w2_words, 2, 3)
-        load_scales(nc.sync, w3_s, w3_scales.rearrange("e s f n -> (e s) f n"), 2, 4)
-        load_scales(nc.sync, w1_s, w1_scales.rearrange("e s f n -> (e s) f n"), 0, 2)
-        load_words("w1", w1_w, w1_words, 0, 1)
-        load_scales(nc.sync, w1_s, w1_scales.rearrange("e s f n -> (e s) f n"), 2, 4)
         load_words("w3", w3_w, w3_words, 0, 1)
+        load_words("w1", w1_w, w1_words, 0, 1)
+        load_scales(nc.sync, w1_s, w1_rows, 0, 4)
         load_words("w2", w2_w, w2_words, 3, 4)
         load_saved("a3", a3_t, a3, 2, 4)
         load_words("w1", w1_w, w1_words, 1, 2)
@@ -98,128 +113,100 @@ def tile_moe_bdx_glu_silu_kernel(
 
         g_w, g_s = {}, {}
 
-        def gather(lo, hi, tag):
+        def gather_scales(lo, hi, passes=range(PASSES)):
             picks = offsets[:, lo * LIST_COLS : hi * LIST_COLS]
-            for s in range(PASSES):
-                scales = keep.tile([P, (hi - lo) * C], U8, name="g_s_%s_%d" % (tag, s), align_bytes=64)
+            for s in passes:
+                scales = v_tile([P, (hi - lo) * C], U8)
                 nc.vector.tensor_copy(scales[:], dy_s[:, s, :].indirect(picks))
                 for e in range(lo, hi):
                     g_s[e, s] = scales[:, (e - lo) * C : (e - lo + 1) * C]
+
+        def gather_words(lo, hi):
+            picks = offsets[:, lo * LIST_COLS : hi * LIST_COLS]
             for s in range(PASSES):
-                words = keep.tile([P, (hi - lo) * C], U32, name="g_w_%s_%d" % (tag, s), align_bytes=64)
+                words = v_tile([P, (hi - lo) * C], U32)
                 nc.vector.tensor_copy(words[:], dy_w[:, s, :].bitcast(U32).indirect(picks))
                 for e in range(lo, hi):
                     g_w[e, s] = words[:, (e - lo) * C : (e - lo + 1) * C]
 
-        windows = [keep.tile([P, T], F32, name="window_%d" % kt, align_bytes=64) for kt in range(KT)]
-        silu_neg, gated_sig, slope, y_ps, dx_ps, dx_sb = {}, {}, {}, {}, {}, {}
+        windows = [place("window_%d" % kt, [P, T], F32) for kt in range(KT)]
+        silu_neg, a1_ps, tanh_half, gated_sig, factor3, factor1, rest = ({} for i in range(7))
+        y_sb, y_ps, dh_ps, da, dx_ps, dx_sb = ({} for i in range(6))
 
         def by_pairs(ap):
             return ap.rearrange("p t (c i) -> p c t i", i=2)
 
-        def functions(e):
-            silu_neg[e] = work.tile([P, 4, C], F32, name="silu_neg", align_bytes=64)
-            nc.scalar.activation(silu_neg[e][:], a1_t[e], ACT.Silu, scale=-1.0)
-            turned = ps_early.tile([P, 4, P], F32, name="early")
+        def function(func, src, **affine):
+            result = s_tile([P, 4, C], F32)[:]
+            nc.scalar.activation(result, src, func, **affine)
+            return result
+
+        def turn(src):
+            turned = bank([P, 4, P])
             for t in range(4):
-                nc.tensor.transpose(turned[:, t, :], a1_t[e][:, t, :], ident[:])
-            tanh_half = work.tile([P, 4, P], F32, name="tanh_half", align_bytes=64)
-            nc.scalar.activation(tanh_half[:], turned[:], ACT.Tanh, scale=0.5)
-            if e == 0:
-                gate_ps = ps_early.tile([P, 4, P], F32, name="early")
-                nc.tensor.transpose(gate_ps[:, 0, :], gate_rows[:], ident[:])
-                nc.scalar.activation(gate_half[:], gate_ps[:, 0, 0:E], ACT.Copy, scale=0.5)
-            gated_sig[e] = work.tile([P, 4, P], F32, name="gated_sig", align_bytes=64)
-            half = gate_half[:, e : e + 1]
-            nc.scalar.activation(gated_sig[e][:], tanh_half[:], ACT.Identity, scale=half, bias=half)
-
-        rests = {}
-
-        def make_rest(e):
-            if e == 0:
-                rest = work.tile([P, 4, C], F32, name="rest", align_bytes=64)
-                nc.scalar.activation(rest[:], silu_neg[e][:], ACT.Copy, scale=-1.0, bias=1.0)
-            else:
-                at = (16384, 0, 2048)[e - 1]
-                rest = reused.tile([P, 4, C], F32, name="rest_%d" % e, align_bytes=64, offset=at)
-                nc.gpsimd.tensor_scalar(rest[:], silu_neg[e][:], -1.0, 1.0, ALU.mult, ALU.add)
-            rests[e] = rest
-
-        def make_slope(e):
-            if e % 2 == 0:
-                slope[e] = reused.tile([P, 4, C], F32, name="slope_%d" % e, align_bytes=64, offset=(12288, 4096)[e // 2])
-            else:
-                slope[e] = work.tile([P, 4, C], F32, name="slope", align_bytes=64)
-            nc.gpsimd.tensor_tensor(slope[e][:], rests[e][:], a3_t[e], ALU.mult)
+                nc.tensor.transpose(turned[:, t, :], src[:, t, :], ident[:])
+            return turned[:]
 
         def first_product(e):
-            dh_ps = ps_dh.tile([P, H], F32, name="dh_ps")
+            sums = bank([P, H])
             for s in range(PASSES):
                 nc.tensor.matmul_mx(
-                    dh_ps[:], lhsT=g_w[e, s].bitcast(FP8X4), lhsT_scale=g_s[e, s],
+                    sums[:], lhsT=g_w[e, s].bitcast(FP8X4), lhsT_scale=g_s[e, s],
                     rhs=w2_w[e][:, s, :].bitcast(FP4X4), rhs_scale=w2_s[:, e * PASSES + s, :],
                     start=(s == 0), stop=(s == PASSES - 1),
                 )
-            if e == 2:
-                y_sb = reused.tile([P, 4, P], F32, name="y_sb_2", align_bytes=64, offset=6144)
-            else:
-                y_sb = work.tile([P, 4, P], F32, name="y_sb", align_bytes=64)
-            nc.vector.tensor_tensor(y_sb[:], dh_ps[:].rearrange("c (p t) -> c t p", t=4), gated_sig[e][:], ALU.mult)
-            y_ps[e] = ps_y.tile([P, 4, C], F32, name="y_ps")
-            for t in range(4):
-                nc.tensor.transpose(y_ps[e][:, t, :], y_sb[:, t, :], ident[:])
+            dh_ps[e] = sums[:].rearrange("c (p t) -> c t p", t=4)
 
-        dx_whole = {}
+        def negative_silu(e):
+            silu_neg[e] = function(ACT.Silu, a1_t[e], scale=-1.0)
+
+        def gate_sigmoid(e):
+            half = gate_half[:, e : e + 1]
+            gated_sig[e] = function(ACT.Identity, tanh_half[e], scale=half, bias=half)
+
+        def make_y(e):
+            y_sb[e] = v_tile([P, 4, P], F32)[:]
+            nc.vector.tensor_tensor(y_sb[e], dh_ps[e], gated_sig[e], ALU.mult)
+
+        def make_rest(e, at):
+            rest[e] = place("rest_%d" % e, [P, 4, C], F32, at)[:]
+            nc.gpsimd.tensor_scalar(rest[e], silu_neg[e], -1.0, 1.0, ALU.mult, ALU.add)
+
+        def make_slope(e, at=None):
+            factor1[e] = place("slope_%d" % e, [P, 4, C], F32, at)[:]
+            nc.gpsimd.tensor_tensor(factor1[e], rest[e], a3_t[e], ALU.mult)
+
+        def make_da(e, which, at=None):
+            if which == 0:
+                da[e] = v_tile([P, 2, C, 4], BF16) if at is None else place("da_%d" % e, [P, 2, C, 4], BF16, at)
+            factor = (factor3, factor1)[which][e]
+            nc.vector.tensor_tensor(
+                da[e][:, which].rearrange("p (c i) t -> p c t i", i=2), by_pairs(y_ps[e]), by_pairs(factor), ALU.mult
+            )
 
         def second_product(e):
-            if e < 2:
-                da = reused.tile([P, 2, C, 4], BF16, name="da_%d" % e, align_bytes=64, offset=(1024, 4096)[e])
-            else:
-                da = reused.tile([P, 2, C, 4], BF16, name="da_%d" % e, align_bytes=64, offset=8192 + 2048 * (e - 2))
-            for which, factor in enumerate((a1_t[e], slope[e][:])):
-                nc.vector.tensor_tensor(
-                    da[:, which].rearrange("p (c i) t -> p c t i", i=2), by_pairs(y_ps[e][:]), by_pairs(factor), ALU.mult
-                )
-            if e == 0:
-                codes = reused.tile([P, 2 * C], U32, name="codes_0", align_bytes=64, offset=6144)
-            else:
-                codes = work.tile([P, 2 * C], U32, name="codes", align_bytes=64)
-            da_s = work.tile([P, 2 * C], U8, name="da_s", align_bytes=64)
-            if e == 0:
-                nc.vector.quantize_mx(codes[:].bitcast(FP8X4), da_s[:], da[:].rearrange("p w j t -> p (w j t)"))
-            else:
-                for which in range(2):
-                    cols = slice(which * C, (which + 1) * C)
-                    nc.vector.quantize_mx(codes[:, cols].bitcast(FP8X4), da_s[:, cols], da[:, which].rearrange("p j t -> p (j t)"))
-
-            if e == 2:
-                dx_whole[e] = ps_early.tile([P, KT, C], F32, name="early")
-                dx_ps[e] = [dx_whole[e][:, 0:2, :], dx_whole[e][:, 2:4, :]]
-            elif e == 3:
-                dx_ps[e] = [ps_early.tile([P, 2, C], F32, name="early")[:], ps_dx.tile([P, 2, C], F32, name="dx_ps")[:]]
-            else:
-                dx_ps[e] = [ps_dx.tile([P, 2, C], F32, name="dx_ps")[:] for h in range(2)]
-            for kt in range(KT):
-                for which, (words, plane) in enumerate(((w3_w, w3_s), (w1_w, w1_s))):
+            codes = v_tile([P, 2 * C], U32)
+            da_s = place("da_s_%d" % e, [P, 2 * C], U8)
+            nc.vector.quantize_mx(codes[:].bitcast(FP8X4), da_s[:], da[e][:].rearrange("p w j t -> p (w j t)"))
+            dx_ps[e] = [bank([P, 2, C])[:] for h in range(2)]
+            for which, (words, plane) in enumerate(((w3_w, w3_s), (w1_w, w1_s))):
+                for kt in range(KT):
                     nc.tensor.matmul_mx(
                         dx_ps[e][kt // 2][:, kt % 2, :],
                         lhsT=words[e][:, 0, kt * 256 : (kt + 1) * 256].bitcast(FP4X4),
                         lhsT_scale=plane[:, e, kt * P : (kt + 1) * P],
                         rhs=codes[:, which * C : (which + 1) * C].bitcast(FP8X4),
                         rhs_scale=da_s[:, which * C : (which + 1) * C],
-                        start=(which == 0), stop=(which == 1),
+                        start=(which == 0 and kt % 2 == 0), stop=(which == 1 and kt % 2 == 1),
                     )
 
         def copy_out(e, h, on_scalar):
-            if (e, h) == (1, 1):
-                t = reused.tile([P, 2, C], F32, name="dx_sb_late", align_bytes=64, offset=10240)
-            else:
-                t = keep.tile([P, 2, C], F32, name="dx_sb_%d_%d" % (e, h), align_bytes=64)
-            dx_sb[e, h] = t[:]
             if on_scalar:
-                nc.scalar.copy(t[:], dx_ps[e][h])
+                dx_sb[e, h] = s_tile([P, 2, C], F32)[:]
+                nc.scalar.copy(dx_sb[e, h], dx_ps[e][h])
             else:
-                nc.vector.tensor_copy(t[:], dx_ps[e][h])
+                dx_sb[e, h] = v_tile([P, 2, C], F32)[:]
+                nc.vector.tensor_copy(dx_sb[e, h], dx_ps[e][h])
 
         def scatter(e, kt, on_scalar):
             picks = offsets[:, e * LIST_COLS : (e + 1) * LIST_COLS]
@@ -228,48 +215,92 @@ def tile_moe_bdx_glu_silu_kernel(
             else:
                 nc.vector.tensor_copy(windows[kt][:].indirect(picks), dx_sb[e, kt // 2][:, kt % 2, :])
             if e == E - 1:
-                queue = nc.scalar if kt == 3 else nc.sync
+                queue = nc.scalar if on_scalar else nc.sync
                 queue.dma_start(out=out[kt * P : (kt + 1) * P, :], in_=windows[kt][:])
 
-        gather(0, 1, "outer")
-        gather(1, 3, "inner")
-        functions(0)
-        make_rest(0)
+        for q in range(4):
+            nc.vector.tensor_copy(dy_s[32 * q : 32 * q + 4].bitcast(I32), dy_s_rows[:, :, q, :].bitcast(I32))
+        gather_scales(0, 1)
+        gather_scales(1, 4, (0,))
+        gather_words(0, 1)
+        gather_scales(1, 4, (1,))
+        gather_words(1, 4)
+
+        negative_silu(0)
+        tanh_half[0] = function(ACT.Tanh, a1_t[0], scale=0.5)
+        gate_ps = bank([P, P])
+        nc.tensor.transpose(gate_ps[:], gate_rows[:], ident[:])
+        a1_ps[1] = turn(a1_t[1])
+        factor3[0] = function(ACT.Silu, a1_t[0])
+        gate_0 = s_tile([P, 1], F32)
+        nc.scalar.copy(gate_0[:], gate_ps[:, 0:1])
+        gate_half = s_tile([P, E], F32)
+        nc.scalar.activation(gate_half[:], gate_ps[:, 0:E], ACT.Copy, scale=0.5)
+        make_rest(0, None)
+        sig_0 = place("sig_0", [P, 4, C], F32, 20 * KB)
+        nc.gpsimd.tensor_scalar(sig_0[:], tanh_half[0], 0.5, 0.5, ALU.mult, ALU.add)
+        part_0 = place("part_0", [P, 4, C], F32, 16 * KB)
+        nc.gpsimd.tensor_tensor(part_0[:], rest[0], sig_0[:], ALU.mult)
+        negative_silu(1)
+        make_rest(1, 20 * KB)
+        factor1[0] = place("factor1_0", [P, 4, C], F32)[:]
+        nc.gpsimd.tensor_tensor(factor1[0], part_0[:], a3_t[0], ALU.mult)
+        make_slope(1, 16 * KB)
+        tanh_half[1] = function(ACT.Tanh, a1_ps[1], scale=0.5)
+        gate_sigmoid(1)
         first_product(0)
-        gather(3, 4, "outer")
-        make_slope(0)
-        functions(1)
-        make_rest(1)
-        make_slope(1)
-        for e in range(2, E):
-            functions(e)
+        y_sb[0] = function(ACT.Copy, dh_ps[0], scale=gate_0[:])
+        a1_ps[2] = turn(a1_t[2])
+        y_ps[0] = turn(y_sb[0])
         first_product(1)
+        make_da(0, 0, 1 * KB)
+        make_da(0, 1)
+        negative_silu(2)
+        tanh_half[2] = function(ACT.Tanh, a1_ps[2], scale=0.5)
+        gate_sigmoid(2)
+        for e in range(1, E):
+            factor3[e] = a1_t[e]
+        negative_silu(3)
+        a1_ps[3] = turn(a1_t[3])
+        tanh_half[3] = function(ACT.Tanh, a1_ps[3], scale=0.5)
+        gate_sigmoid(3)
+        first_product(2)
+        make_y(1)
+        y_ps[1] = turn(y_sb[1])
         second_product(0)
         for h in range(2):
             copy_out(0, h, True)
             scatter(0, 2 * h, True)
             scatter(0, 2 * h + 1, True)
-        make_rest(2)
-        make_rest(3)
-        first_product(2)
-        second_product(1)
-        make_slope(2)
-        make_slope(3)
+        make_y(2)
+        y_ps[2] = turn(y_sb[2])
         first_product(3)
-        copy_out(1, 0, True)
-        for kt in (0, 1):
-            scatter(1, kt, True)
+        make_rest(2, 0)
+        make_rest(3, 2 * KB)
+        make_da(1, 0, 12 * KB)
+        make_da(1, 1)
+        second_product(1)
+        make_slope(2, 12 * KB)
+        make_slope(3, 0)
+        make_y(3)
+        y_ps[3] = turn(y_sb[3])
+        make_da(2, 0)
+        make_da(2, 1)
+        make_da(3, 0)
         second_product(2)
+        make_da(3, 1)
         second_product(3)
-        copy_out(1, 1, False)
-        for kt in (2, 3):
-            scatter(1, kt, False)
-        dx_2 = keep.tile([P, KT, C], F32, name="dx_sb_2", align_bytes=64)
-        nc.scalar.copy(dx_2[:], dx_whole[2][:])
-        dx_sb[2, 0], dx_sb[2, 1] = dx_2[:, 0:2, :], dx_2[:, 2:4, :]
-        for kt in range(KT):
-            scatter(2, kt, True)
+        for h in (1, 0):
+            copy_out(1, h, True)
+            scatter(1, 2 * h, True)
+            scatter(1, 2 * h + 1, True)
+        for e in (2, 3):
+            copy_out(e, 1, False)
+            scatter(e, 2, False)
+            scatter(e, 3, False)
+        copy_out(2, 0, True)
+        scatter(2, 0, True)
+        scatter(2, 1, True)
         copy_out(3, 0, False)
-        copy_out(3, 1, True)
-        for kt in range(KT):
-            scatter(3, kt, kt == 3)
+        scatter(3, 0, False)
+        scatter(3, 1, True)

@@ -50,19 +50,22 @@ def tile_moe_bdx_glu_silu_kernel(
             return reused.tile(shape, dtype, name=name, align_bytes=64, offset=at)
 
         offsets = keep.tile([P, E * LIST_COLS], U16, name="offsets")
-        dy_w = place("dy_w", [P, PASSES, T], I32)
+        dy_w = place("dy_w", [P, PASSES, T], I32, 24 * KB)
         dy_s = place("dy_s", [P, PASSES, T], U8)
         dy_s_rows = place("dy_s_rows", [4, PASSES, 4, T], U8)
-        w2_s = place("w2_s", [P, E * PASSES, H], U8)
-        w1_s = place("w1_s", [P, E, K], U8)
-        w3_s = place("w3_s", [P, E, K], U8)
         ident = place("ident", [P, P], F32)
         gate_rows = place("gate_rows", [P, C], F32)
 
-        def load_scales(queue, plane, rows, lo=0, hi=4):
-            by_row = rows.rearrange("a (q r) n -> r q a n", r=4)
-            for r in range(lo, hi):
-                queue.dma_start(out=plane[r:P:32, :, :].bitcast(I32), in_=by_row[r].bitcast(I32))
+        w2_s, w1_s, w3_s = {}, {}, {}
+
+        def load_scales(name, table, src, lo, hi):
+            passes = src.shape[1]
+            plane = place("%s_s_%d" % (name, lo), [P, (hi - lo) * passes, 512], U8)
+            by_row = src.rearrange("e s (q r) n -> r q (e s) n", r=4).bitcast(I32)
+            for r in range(4):
+                nc.sync.dma_start(out=plane[r:P:32].bitcast(I32), in_=by_row[r][:, lo * passes : hi * passes, :])
+            for e in range(lo, hi):
+                table[e] = plane[:, (e - lo) * passes : (e - lo + 1) * passes, :]
 
         w2_w, w1_w, w3_w, a1_t, a3_t = {}, {}, {}, {}, {}
 
@@ -80,10 +83,6 @@ def tile_moe_bdx_glu_silu_kernel(
             for e in range(lo, hi):
                 table[e] = t[:, :, (e - lo) * C : (e - lo + 1) * C]
 
-        w2_rows = w2_scales.rearrange("e s f n -> (e s) f n")
-        w1_rows = w1_scales.rearrange("e s f n -> (e s) f n")
-        w3_rows = w3_scales.rearrange("e s f n -> (e s) f n")
-
         nc.gpsimd.memset(dy_s[:].rearrange("p a b -> p (a b)").bitcast(I32), 0)
         nc.gpsimd.memset(gate_rows[:], 0.0)
         make_identity(nc, ident[:])
@@ -91,19 +90,18 @@ def tile_moe_bdx_glu_silu_kernel(
         nc.scalar.dma_start(out=dy_s_rows[:].rearrange("r s q n -> r (s q) n").bitcast(I32), in_=dy_scales.rearrange("s (q r) n -> r (s q) n", r=4).bitcast(I32))
         load_saved("a1", a1_t, a1, 0, 1)
         nc.sync.dma_start(out=gate_rows[0:E, :], in_=gate[0].rearrange("(e c) -> e c", e=E))
-        load_saved("a1", a1_t, a1, 1, 2)
         nc.sync.dma_start(out=dy_w[:], in_=dy_words.rearrange("s p t d -> p s (t d)").bitcast(I32))
         load_words("w2", w2_w, w2_words, 0, 1)
-        load_scales(nc.sync, w2_s, w2_rows, 0, 4)
-        load_saved("a1", a1_t, a1, 2, 4)
-        load_saved("a3", a3_t, a3, 0, 1)
+        load_scales("w2", w2_s, w2_scales, 0, 4)
+        load_saved("a1", a1_t, a1, 1, 2)
+        load_saved("a3", a3_t, a3, 0, 2)
         load_words("w2", w2_w, w2_words, 1, 2)
-        load_saved("a3", a3_t, a3, 1, 2)
-        load_scales(nc.sync, w3_s, w3_rows, 0, 4)
-        load_words("w2", w2_w, w2_words, 2, 3)
+        load_saved("a1", a1_t, a1, 2, 4)
+        load_scales("w3", w3_s, w3_scales, 0, 4)
         load_words("w3", w3_w, w3_words, 0, 1)
         load_words("w1", w1_w, w1_words, 0, 1)
-        load_scales(nc.sync, w1_s, w1_rows, 0, 4)
+        load_scales("w1", w1_s, w1_scales, 0, 4)
+        load_words("w2", w2_w, w2_words, 2, 3)
         load_words("w2", w2_w, w2_words, 3, 4)
         load_saved("a3", a3_t, a3, 2, 4)
         load_words("w1", w1_w, w1_words, 1, 2)
@@ -113,9 +111,9 @@ def tile_moe_bdx_glu_silu_kernel(
 
         g_w, g_s = {}, {}
 
-        def gather_scales(lo, hi, passes=range(PASSES)):
+        def gather_scales(lo, hi):
             picks = offsets[:, lo * LIST_COLS : hi * LIST_COLS]
-            for s in passes:
+            for s in range(PASSES):
                 scales = v_tile([P, (hi - lo) * C], U8)
                 nc.vector.tensor_copy(scales[:], dy_s[:, s, :].indirect(picks))
                 for e in range(lo, hi):
@@ -130,7 +128,7 @@ def tile_moe_bdx_glu_silu_kernel(
                     g_w[e, s] = words[:, (e - lo) * C : (e - lo + 1) * C]
 
         windows = [place("window_%d" % kt, [P, T], F32) for kt in range(KT)]
-        silu_neg, a1_ps, tanh_half, gated_sig, factor3, factor1, rest = ({} for i in range(7))
+        silu_neg, a1_ps, tanh_half, gated_sig, factor1, rest = ({} for i in range(6))
         y_sb, y_ps, dh_ps, da, dx_ps, dx_sb = ({} for i in range(6))
 
         def by_pairs(ap):
@@ -152,7 +150,7 @@ def tile_moe_bdx_glu_silu_kernel(
             for s in range(PASSES):
                 nc.tensor.matmul_mx(
                     sums[:], lhsT=g_w[e, s].bitcast(FP8X4), lhsT_scale=g_s[e, s],
-                    rhs=w2_w[e][:, s, :].bitcast(FP4X4), rhs_scale=w2_s[:, e * PASSES + s, :],
+                    rhs=w2_w[e][:, s, :].bitcast(FP4X4), rhs_scale=w2_s[e][:, s, :],
                     start=(s == 0), stop=(s == PASSES - 1),
                 )
             dh_ps[e] = sums[:].rearrange("c (p t) -> c t p", t=4)
@@ -168,10 +166,6 @@ def tile_moe_bdx_glu_silu_kernel(
             y_sb[e] = v_tile([P, 4, P], F32)[:]
             nc.vector.tensor_tensor(y_sb[e], dh_ps[e], gated_sig[e], ALU.mult)
 
-        def make_rest(e, at):
-            rest[e] = place("rest_%d" % e, [P, 4, C], F32, at)[:]
-            nc.gpsimd.tensor_scalar(rest[e], silu_neg[e], -1.0, 1.0, ALU.mult, ALU.add)
-
         def make_slope(e, at=None):
             factor1[e] = place("slope_%d" % e, [P, 4, C], F32, at)[:]
             nc.gpsimd.tensor_tensor(factor1[e], rest[e], a3_t[e], ALU.mult)
@@ -179,7 +173,7 @@ def tile_moe_bdx_glu_silu_kernel(
         def make_da(e, which, at=None):
             if which == 0:
                 da[e] = v_tile([P, 2, C, 4], BF16) if at is None else place("da_%d" % e, [P, 2, C, 4], BF16, at)
-            factor = (factor3, factor1)[which][e]
+            factor = (a1_t, factor1)[which][e]
             nc.vector.tensor_tensor(
                 da[e][:, which].rearrange("p (c i) t -> p c t i", i=2), by_pairs(y_ps[e]), by_pairs(factor), ALU.mult
             )
@@ -194,7 +188,7 @@ def tile_moe_bdx_glu_silu_kernel(
                     nc.tensor.matmul_mx(
                         dx_ps[e][kt // 2][:, kt % 2, :],
                         lhsT=words[e][:, 0, kt * 256 : (kt + 1) * 256].bitcast(FP4X4),
-                        lhsT_scale=plane[:, e, kt * P : (kt + 1) * P],
+                        lhsT_scale=plane[e][:, 0, kt * P : (kt + 1) * P],
                         rhs=codes[:, which * C : (which + 1) * C].bitcast(FP8X4),
                         rhs_scale=da_s[:, which * C : (which + 1) * C],
                         start=(which == 0 and kt % 2 == 0), stop=(which == 1 and kt % 2 == 1),
@@ -220,51 +214,45 @@ def tile_moe_bdx_glu_silu_kernel(
 
         for q in range(4):
             nc.vector.tensor_copy(dy_s[32 * q : 32 * q + 4].bitcast(I32), dy_s_rows[:, :, q, :].bitcast(I32))
-        gather_scales(0, 1)
-        gather_scales(1, 4, (0,))
+        gather_scales(0, 2)
         gather_words(0, 1)
-        gather_scales(1, 4, (1,))
-        gather_words(1, 4)
+        gather_words(1, 2)
+        gather_scales(2, 4)
 
         negative_silu(0)
-        tanh_half[0] = function(ACT.Tanh, a1_t[0], scale=0.5)
+        a1_ps[0] = turn(a1_t[0])
         gate_ps = bank([P, P])
         nc.tensor.transpose(gate_ps[:], gate_rows[:], ident[:])
-        a1_ps[1] = turn(a1_t[1])
-        factor3[0] = function(ACT.Silu, a1_t[0])
-        gate_0 = s_tile([P, 1], F32)
-        nc.scalar.copy(gate_0[:], gate_ps[:, 0:1])
+        tanh_half[0] = function(ACT.Tanh, a1_ps[0], scale=0.5)
         gate_half = s_tile([P, E], F32)
         nc.scalar.activation(gate_half[:], gate_ps[:, 0:E], ACT.Copy, scale=0.5)
-        make_rest(0, None)
-        sig_0 = place("sig_0", [P, 4, C], F32, 20 * KB)
-        nc.gpsimd.tensor_scalar(sig_0[:], tanh_half[0], 0.5, 0.5, ALU.mult, ALU.add)
-        part_0 = place("part_0", [P, 4, C], F32, 16 * KB)
-        nc.gpsimd.tensor_tensor(part_0[:], rest[0], sig_0[:], ALU.mult)
+        gate_sigmoid(0)
+        rest[0] = place("rest_0", [P, 4, C], F32, 16 * KB)[:]
+        nc.scalar.activation(rest[0], silu_neg[0], ACT.Copy, scale=-1.0, bias=1.0)
+        first_product(0)
+        a1_ps[1] = turn(a1_t[1])
         negative_silu(1)
-        make_rest(1, 20 * KB)
-        factor1[0] = place("factor1_0", [P, 4, C], F32)[:]
-        nc.gpsimd.tensor_tensor(factor1[0], part_0[:], a3_t[0], ALU.mult)
-        make_slope(1, 16 * KB)
         tanh_half[1] = function(ACT.Tanh, a1_ps[1], scale=0.5)
         gate_sigmoid(1)
-        first_product(0)
-        y_sb[0] = function(ACT.Copy, dh_ps[0], scale=gate_0[:])
-        a1_ps[2] = turn(a1_t[2])
+        make_y(0)
         y_ps[0] = turn(y_sb[0])
+        factor1[0] = v_tile([P, 4, C], F32)[:]
+        nc.vector.tensor_tensor(factor1[0], rest[0], a3_t[0], ALU.mult)
         first_product(1)
-        make_da(0, 0, 1 * KB)
-        make_da(0, 1)
-        negative_silu(2)
+        late_neg = place("late_neg", [P, 2, 4, C], F32)
+        a1_ps[2] = turn(a1_t[2])
         tanh_half[2] = function(ACT.Tanh, a1_ps[2], scale=0.5)
+        nc.scalar.activation(late_neg[:, 0], a1_t[2], ACT.Silu, scale=-1.0)
         gate_sigmoid(2)
-        for e in range(1, E):
-            factor3[e] = a1_t[e]
-        negative_silu(3)
         a1_ps[3] = turn(a1_t[3])
         tanh_half[3] = function(ACT.Tanh, a1_ps[3], scale=0.5)
+        nc.scalar.activation(late_neg[:, 1], a1_t[3], ACT.Silu, scale=-1.0)
         gate_sigmoid(3)
-        first_product(2)
+        rest[1] = place("rest_1", [P, 4, C], F32, 16 * KB)[:]
+        nc.gpsimd.tensor_scalar(rest[1], silu_neg[1], -1.0, 1.0, ALU.mult, ALU.add)
+        make_slope(1)
+        make_da(0, 0)
+        make_da(0, 1)
         make_y(1)
         y_ps[1] = turn(y_sb[1])
         second_product(0)
@@ -272,16 +260,19 @@ def tile_moe_bdx_glu_silu_kernel(
             copy_out(0, h, True)
             scatter(0, 2 * h, True)
             scatter(0, 2 * h + 1, True)
-        make_y(2)
-        y_ps[2] = turn(y_sb[2])
+        gather_words(2, 4)
+        first_product(2)
         first_product(3)
-        make_rest(2, 0)
-        make_rest(3, 2 * KB)
+        late_rest = place("late_rest", [P, 2, 4, C], F32, 24 * KB)
+        nc.gpsimd.tensor_scalar(late_rest[:], late_neg[:], -1.0, 1.0, ALU.mult, ALU.add)
+        rest[2], rest[3] = late_rest[:, 0], late_rest[:, 1]
         make_da(1, 0, 12 * KB)
         make_da(1, 1)
+        make_y(2)
+        y_ps[2] = turn(y_sb[2])
         second_product(1)
-        make_slope(2, 12 * KB)
-        make_slope(3, 0)
+        make_slope(2, 11 * KB)
+        make_slope(3, 13 * KB)
         make_y(3)
         y_ps[3] = turn(y_sb[3])
         make_da(2, 0)

@@ -22,6 +22,7 @@ PASSES = N // 512
 KT = K // P
 LIST_COLS = C // 16
 KB = 1024
+LAST_WINDOW = 3
 
 
 def tile_moe_bdx_glu_silu_kernel(
@@ -31,7 +32,7 @@ def tile_moe_bdx_glu_silu_kernel(
     with ExitStack() as ctx:
         keep = ctx.enter_context(tc.tile_pool(name="keep", bufs=1))
         reused = ctx.enter_context(tc.tile_pool(name="reused", bufs=1))
-        by_vector = ctx.enter_context(tc.tile_pool(name="by_vector", bufs=28))
+        by_vector = ctx.enter_context(tc.tile_pool(name="by_vector", bufs=36))
         by_scalar = ctx.enter_context(tc.tile_pool(name="by_scalar", bufs=24))
         banks = ctx.enter_context(tc.psum_pool(name="banks", bufs=8))
 
@@ -52,20 +53,27 @@ def tile_moe_bdx_glu_silu_kernel(
         offsets = keep.tile([P, E * LIST_COLS], U16, name="offsets")
         dy_w = place("dy_w", [P, PASSES, T], I32, 24 * KB)
         dy_s = place("dy_s", [P, PASSES, T], U8)
-        dy_s_rows = place("dy_s_rows", [4, PASSES, 4, T], U8)
         ident = place("ident", [P, P], F32)
         gate_rows = place("gate_rows", [P, C], F32)
+
+        def load_rows(queue, plane, rows, lo, hi):
+            for r in range(lo, hi):
+                queue.dma_start(out=plane[r:P:32].bitcast(I32), in_=rows[r])
+
+        def by_row(src):
+            return src.rearrange("a (q r) n -> r q a n", r=4).bitcast(I32)
 
         w2_s, w1_s, w3_s = {}, {}, {}
 
         def load_scales(name, table, src, lo, hi):
             passes = src.shape[1]
             plane = place("%s_s_%d" % (name, lo), [P, (hi - lo) * passes, 512], U8)
-            by_row = src.rearrange("e s (q r) n -> r q (e s) n", r=4).bitcast(I32)
-            for r in range(4):
-                nc.sync.dma_start(out=plane[r:P:32].bitcast(I32), in_=by_row[r][:, lo * passes : hi * passes, :])
+            rows = by_row(src.rearrange("e s f n -> (e s) f n"))
+            load_rows(nc.sync, plane, rows[:, :, lo * passes : hi * passes, :], 0, 4)
             for e in range(lo, hi):
                 table[e] = plane[:, (e - lo) * passes : (e - lo + 1) * passes, :]
+
+        dy_rows = by_row(dy_scales)
 
         w2_w, w1_w, w3_w, a1_t, a3_t = {}, {}, {}, {}, {}
 
@@ -87,21 +95,23 @@ def tile_moe_bdx_glu_silu_kernel(
         nc.gpsimd.memset(gate_rows[:], 0.0)
         make_identity(nc, ident[:])
         nc.sync.dma_start(offsets[:], offs)
-        nc.scalar.dma_start(out=dy_s_rows[:].rearrange("r s q n -> r (s q) n").bitcast(I32), in_=dy_scales.rearrange("s (q r) n -> r (s q) n", r=4).bitcast(I32))
+        load_rows(nc.scalar, dy_s, dy_rows, 0, 2)
         load_saved("a1", a1_t, a1, 0, 1)
+        load_rows(nc.sync, dy_s, dy_rows, 2, 4)
         nc.sync.dma_start(out=gate_rows[0:E, :], in_=gate[0].rearrange("(e c) -> e c", e=E))
         nc.sync.dma_start(out=dy_w[:], in_=dy_words.rearrange("s p t d -> p s (t d)").bitcast(I32))
         load_words("w2", w2_w, w2_words, 0, 1)
-        load_scales("w2", w2_s, w2_scales, 0, 4)
+        load_scales("w2", w2_s, w2_scales, 0, 2)
         load_saved("a1", a1_t, a1, 1, 2)
-        load_saved("a3", a3_t, a3, 0, 2)
         load_words("w2", w2_w, w2_words, 1, 2)
+        load_saved("a3", a3_t, a3, 0, 2)
         load_saved("a1", a1_t, a1, 2, 4)
+        load_scales("w2", w2_s, w2_scales, 2, 4)
+        load_words("w2", w2_w, w2_words, 2, 3)
         load_scales("w3", w3_s, w3_scales, 0, 4)
         load_words("w3", w3_w, w3_words, 0, 1)
         load_words("w1", w1_w, w1_words, 0, 1)
         load_scales("w1", w1_s, w1_scales, 0, 4)
-        load_words("w2", w2_w, w2_words, 2, 3)
         load_words("w2", w2_w, w2_words, 3, 4)
         load_saved("a3", a3_t, a3, 2, 4)
         load_words("w1", w1_w, w1_words, 1, 2)
@@ -129,7 +139,7 @@ def tile_moe_bdx_glu_silu_kernel(
 
         windows = [place("window_%d" % kt, [P, T], F32) for kt in range(KT)]
         silu_neg, a1_ps, tanh_half, gated_sig, factor1, rest = ({} for i in range(6))
-        y_sb, y_ps, dh_ps, da, dx_ps, dx_sb = ({} for i in range(6))
+        y_sb, y_ps, dh_ps, da, da_mx, dx_ps, dx_sb = ({} for i in range(7))
 
         def by_pairs(ap):
             return ap.rearrange("p t (c i) -> p c t i", i=2)
@@ -162,36 +172,55 @@ def tile_moe_bdx_glu_silu_kernel(
             half = gate_half[:, e : e + 1]
             gated_sig[e] = function(ACT.Identity, tanh_half[e], scale=half, bias=half)
 
+        def spread_gate():
+            gate_ps = bank([P, P])
+            nc.tensor.transpose(gate_ps[:], gate_rows[:], ident[:])
+            half = s_tile([P, E], F32)
+            nc.scalar.activation(half[:], gate_ps[:, 0:E], ACT.Copy, scale=0.5)
+            return half
+
         def make_y(e):
             y_sb[e] = v_tile([P, 4, P], F32)[:]
             nc.vector.tensor_tensor(y_sb[e], dh_ps[e], gated_sig[e], ALU.mult)
+
+        def make_rest(e, at=None, on_scalar=False):
+            rest[e] = place("rest_%d" % e, [P, 4, C], F32, at)[:]
+            if on_scalar:
+                nc.scalar.activation(rest[e], silu_neg[e], ACT.Copy, scale=-1.0, bias=1.0)
+            else:
+                nc.gpsimd.tensor_scalar(rest[e], silu_neg[e], -1.0, 1.0, ALU.mult, ALU.add)
+
+        def sigmoid_part(e):
+            tanh_half[e] = function(ACT.Tanh, a1_ps[e], scale=0.5)
 
         def make_slope(e, at=None):
             factor1[e] = place("slope_%d" % e, [P, 4, C], F32, at)[:]
             nc.gpsimd.tensor_tensor(factor1[e], rest[e], a3_t[e], ALU.mult)
 
         def make_da(e, which, at=None):
-            if which == 0:
-                da[e] = v_tile([P, 2, C, 4], BF16) if at is None else place("da_%d" % e, [P, 2, C, 4], BF16, at)
+            da[e, which] = v_tile([P, C, 4], BF16) if at is None else place("da_%d_%d" % (e, which), [P, C, 4], BF16, at)
             factor = (a1_t, factor1)[which][e]
             nc.vector.tensor_tensor(
-                da[e][:, which].rearrange("p (c i) t -> p c t i", i=2), by_pairs(y_ps[e]), by_pairs(factor), ALU.mult
+                da[e, which][:].rearrange("p (c i) t -> p c t i", i=2), by_pairs(y_ps[e]), by_pairs(factor), ALU.mult
             )
 
+        def quantize(e, which):
+            codes = v_tile([P, C], U32)
+            da_s = place("da_s_%d_%d" % (e, which), [P, C], U8)
+            nc.vector.quantize_mx(codes[:].bitcast(FP8X4), da_s[:], da[e, which][:].rearrange("p j t -> p (j t)"))
+            da_mx[e, which] = codes, da_s
+
         def second_product(e):
-            codes = v_tile([P, 2 * C], U32)
-            da_s = place("da_s_%d" % e, [P, 2 * C], U8)
-            nc.vector.quantize_mx(codes[:].bitcast(FP8X4), da_s[:], da[e][:].rearrange("p w j t -> p (w j t)"))
             dx_ps[e] = [bank([P, 2, C])[:] for h in range(2)]
-            for which, (words, plane) in enumerate(((w3_w, w3_s), (w1_w, w1_s))):
-                for kt in range(KT):
+            for kt in range(KT):
+                for which, (words, plane) in enumerate(((w3_w, w3_s), (w1_w, w1_s))):
+                    codes, da_s = da_mx[e, which]
                     nc.tensor.matmul_mx(
                         dx_ps[e][kt // 2][:, kt % 2, :],
                         lhsT=words[e][:, 0, kt * 256 : (kt + 1) * 256].bitcast(FP4X4),
                         lhsT_scale=plane[e][:, 0, kt * P : (kt + 1) * P],
-                        rhs=codes[:, which * C : (which + 1) * C].bitcast(FP8X4),
-                        rhs_scale=da_s[:, which * C : (which + 1) * C],
-                        start=(which == 0 and kt % 2 == 0), stop=(which == 1 and kt % 2 == 1),
+                        rhs=codes[:].bitcast(FP8X4), rhs_scale=da_s[:],
+                        start=(which == 0), stop=(which == 1),
                     )
 
         def copy_out(e, h, on_scalar):
@@ -209,89 +238,92 @@ def tile_moe_bdx_glu_silu_kernel(
             else:
                 nc.vector.tensor_copy(windows[kt][:].indirect(picks), dx_sb[e, kt // 2][:, kt % 2, :])
             if e == E - 1:
-                queue = nc.scalar if on_scalar else nc.sync
+                queue = nc.scalar if kt == LAST_WINDOW else nc.sync
                 queue.dma_start(out=out[kt * P : (kt + 1) * P, :], in_=windows[kt][:])
 
-        for q in range(4):
-            nc.vector.tensor_copy(dy_s[32 * q : 32 * q + 4].bitcast(I32), dy_s_rows[:, :, q, :].bitcast(I32))
         gather_scales(0, 2)
         gather_words(0, 1)
         gather_words(1, 2)
         gather_scales(2, 4)
-
+        gather_words(2, 4)
         negative_silu(0)
         a1_ps[0] = turn(a1_t[0])
-        gate_ps = bank([P, P])
-        nc.tensor.transpose(gate_ps[:], gate_rows[:], ident[:])
-        tanh_half[0] = function(ACT.Tanh, a1_ps[0], scale=0.5)
-        gate_half = s_tile([P, E], F32)
-        nc.scalar.activation(gate_half[:], gate_ps[:, 0:E], ACT.Copy, scale=0.5)
+        gate_half = spread_gate()
+        sigmoid_part(0)
+        make_rest(0, on_scalar=True)
         gate_sigmoid(0)
-        rest[0] = place("rest_0", [P, 4, C], F32, 16 * KB)[:]
-        nc.scalar.activation(rest[0], silu_neg[0], ACT.Copy, scale=-1.0, bias=1.0)
         first_product(0)
         a1_ps[1] = turn(a1_t[1])
-        negative_silu(1)
-        tanh_half[1] = function(ACT.Tanh, a1_ps[1], scale=0.5)
-        gate_sigmoid(1)
         make_y(0)
-        y_ps[0] = turn(y_sb[0])
-        factor1[0] = v_tile([P, 4, C], F32)[:]
-        nc.vector.tensor_tensor(factor1[0], rest[0], a3_t[0], ALU.mult)
+        negative_silu(1)
+        sigmoid_part(1)
         first_product(1)
-        late_neg = place("late_neg", [P, 2, 4, C], F32)
-        a1_ps[2] = turn(a1_t[2])
-        tanh_half[2] = function(ACT.Tanh, a1_ps[2], scale=0.5)
-        nc.scalar.activation(late_neg[:, 0], a1_t[2], ACT.Silu, scale=-1.0)
-        gate_sigmoid(2)
-        a1_ps[3] = turn(a1_t[3])
-        tanh_half[3] = function(ACT.Tanh, a1_ps[3], scale=0.5)
-        nc.scalar.activation(late_neg[:, 1], a1_t[3], ACT.Silu, scale=-1.0)
-        gate_sigmoid(3)
-        rest[1] = place("rest_1", [P, 4, C], F32, 16 * KB)[:]
-        nc.gpsimd.tensor_scalar(rest[1], silu_neg[1], -1.0, 1.0, ALU.mult, ALU.add)
+        y_ps[0] = turn(y_sb[0])
+        gate_sigmoid(1)
+        make_rest(1, 24 * KB)
+        make_slope(0, 26 * KB)
         make_slope(1)
-        make_da(0, 0)
-        make_da(0, 1)
         make_y(1)
+        a1_ps[2] = turn(a1_t[2])
         y_ps[1] = turn(y_sb[1])
-        second_product(0)
-        for h in range(2):
-            copy_out(0, h, True)
-            scatter(0, 2 * h, True)
-            scatter(0, 2 * h + 1, True)
-        gather_words(2, 4)
+        a1_ps[3] = turn(a1_t[3])
+        sigmoid_part(2)
+        negative_silu(2)
+        gate_sigmoid(2)
+        sigmoid_part(3)
+        negative_silu(3)
+        gate_sigmoid(3)
+        make_da(0, 0)
+        make_da(0, 1, 2 * KB)
         first_product(2)
-        first_product(3)
-        late_rest = place("late_rest", [P, 2, 4, C], F32, 24 * KB)
-        nc.gpsimd.tensor_scalar(late_rest[:], late_neg[:], -1.0, 1.0, ALU.mult, ALU.add)
-        rest[2], rest[3] = late_rest[:, 0], late_rest[:, 1]
-        make_da(1, 0, 12 * KB)
-        make_da(1, 1)
+        make_da(1, 0)
+        quantize(0, 0)
+        quantize(0, 1)
+        second_product(0)
+        make_da(1, 1, 12 * KB)
+        make_rest(2, 1 * KB)
+        make_rest(3, 24 * KB)
         make_y(2)
+        first_product(3)
         y_ps[2] = turn(y_sb[2])
-        second_product(1)
-        make_slope(2, 11 * KB)
-        make_slope(3, 13 * KB)
+        quantize(1, 0)
+        quantize(1, 1)
+        copy_out(0, 0, True)
+        copy_out(0, 1, True)
+        scatter(0, 0, True)
+        scatter(0, 1, True)
+        scatter(0, 2, True)
+        scatter(0, 3, True)
         make_y(3)
         y_ps[3] = turn(y_sb[3])
+        second_product(1)
+        make_slope(2, 11 * KB)
+        make_slope(3, 1 * KB)
         make_da(2, 0)
-        make_da(2, 1)
         make_da(3, 0)
+        make_da(2, 1)
+        copy_out(1, 0, True)
+        quantize(2, 0)
+        quantize(2, 1)
         second_product(2)
         make_da(3, 1)
+        copy_out(1, 1, False)
+        scatter(1, 0, True)
+        scatter(1, 1, True)
+        quantize(3, 0)
+        quantize(3, 1)
         second_product(3)
-        for h in (1, 0):
-            copy_out(1, h, True)
-            scatter(1, 2 * h, True)
-            scatter(1, 2 * h + 1, True)
-        for e in (2, 3):
-            copy_out(e, 1, False)
-            scatter(e, 2, False)
-            scatter(e, 3, False)
+        scatter(1, 2, False)
+        scatter(1, 3, False)
         copy_out(2, 0, True)
+        copy_out(2, 1, True)
         scatter(2, 0, True)
         scatter(2, 1, True)
         copy_out(3, 0, False)
+        copy_out(3, 1, False)
+        scatter(2, 2, True)
+        scatter(2, 3, True)
         scatter(3, 0, False)
-        scatter(3, 1, True)
+        scatter(3, 1, False)
+        scatter(3, 2, False)
+        scatter(3, 3, True)

from contextlib import ExitStack

import concourse.mybir as mybir
from concourse.masks import make_identity

K, T, E, C, H, N = 512, 512, 4, 128, 512, 1024
FLOPS = 2 * E * C * (N * H + 2 * H * K)

F32 = mybir.dt.float32
BF16 = mybir.dt.bfloat16
I32 = mybir.dt.int32
U32 = mybir.dt.uint32
U16 = mybir.dt.uint16
U8 = mybir.dt.uint8
FP8X4 = mybir.dt.float8_e4m3fn_x4
FP4X4 = mybir.dt.float4_e2m1fn_x4
ACT = mybir.ActivationFunctionType
ALU = mybir.AluOpType

P = 128
PASSES = N // 512
KT = K // P
LIST_COLS = C // 16
KB = 1024
LAST_WINDOW = 3


def tile_moe_bdx_glu_silu_kernel(
    tc, dy_words, dy_scales, a1, a3, w2_words, w2_scales, w1_words, w1_scales, w3_words, w3_scales, gate, offs, out
):
    nc = tc.nc
    with ExitStack() as ctx:
        keep = ctx.enter_context(tc.tile_pool(name="keep", bufs=1))
        reused = ctx.enter_context(tc.tile_pool(name="reused", bufs=1))
        by_vector = ctx.enter_context(tc.tile_pool(name="by_vector", bufs=36))
        by_scalar = ctx.enter_context(tc.tile_pool(name="by_scalar", bufs=24))
        banks = ctx.enter_context(tc.psum_pool(name="banks", bufs=8))

        def v_tile(shape, dtype):
            return by_vector.tile(shape, dtype, name="v", align_bytes=64)

        def s_tile(shape, dtype):
            return by_scalar.tile(shape, dtype, name="s", align_bytes=64)

        def bank(shape):
            return banks.tile(shape, F32, name="bank")

        def place(name, shape, dtype, at=None):
            if at is None:
                return keep.tile(shape, dtype, name=name, align_bytes=64)
            return reused.tile(shape, dtype, name=name, align_bytes=64, offset=at)

        offsets = keep.tile([P, E * LIST_COLS], U16, name="offsets")
        dy_w = place("dy_w", [P, PASSES, T], I32, 24 * KB)
        dy_s = place("dy_s", [P, PASSES, T], U8)
        ident = place("ident", [P, P], F32)
        gate_rows = place("gate_rows", [P, C], F32)

        def load_rows(queue, plane, rows, lo, hi):
            for r in range(lo, hi):
                queue.dma_start(out=plane[r:P:32].bitcast(I32), in_=rows[r])

        def by_row(src):
            return src.rearrange("a (q r) n -> r q a n", r=4).bitcast(I32)

        w2_s, w1_s, w3_s = {}, {}, {}

        def load_scales(name, table, src, lo, hi):
            passes = src.shape[1]
            plane = place("%s_s_%d" % (name, lo), [P, (hi - lo) * passes, 512], U8)
            rows = by_row(src.rearrange("e s f n -> (e s) f n"))
            load_rows(nc.sync, plane, rows[:, :, lo * passes : hi * passes, :], 0, 4)
            for e in range(lo, hi):
                table[e] = plane[:, (e - lo) * passes : (e - lo + 1) * passes, :]

        dy_rows = by_row(dy_scales)

        w2_w, w1_w, w3_w, a1_t, a3_t = {}, {}, {}, {}, {}

        def load_words(name, table, src, lo, hi):
            passes = src.shape[1]
            t = place("%s_%d" % (name, lo), [P, (hi - lo) * passes, 1024], U8)
            rows = src.rearrange("e s p b -> p (e s) b").bitcast(I32)
            nc.sync.dma_start(out=t[:].bitcast(I32), in_=rows[:, lo * passes : hi * passes, :])
            for e in range(lo, hi):
                table[e] = t[:, (e - lo) * passes : (e - lo + 1) * passes, :]

        def load_saved(name, table, src, lo, hi):
            t = place("%s_%d" % (name, lo), [P, 4, (hi - lo) * C], F32)
            nc.sync.dma_start(out=t[:], in_=src.rearrange("(p t) j -> p t j", t=4)[:, :, lo * C : hi * C])
            for e in range(lo, hi):
                table[e] = t[:, :, (e - lo) * C : (e - lo + 1) * C]

        nc.gpsimd.memset(dy_s[:].rearrange("p a b -> p (a b)").bitcast(I32), 0)
        nc.gpsimd.memset(gate_rows[:], 0.0)
        make_identity(nc, ident[:])
        nc.sync.dma_start(offsets[:], offs)
        load_rows(nc.scalar, dy_s, dy_rows, 0, 2)
        load_saved("a1", a1_t, a1, 0, 1)
        load_rows(nc.sync, dy_s, dy_rows, 2, 4)
        nc.sync.dma_start(out=gate_rows[0:E, :], in_=gate[0].rearrange("(e c) -> e c", e=E))
        nc.sync.dma_start(out=dy_w[:], in_=dy_words.rearrange("s p t d -> p s (t d)").bitcast(I32))
        load_words("w2", w2_w, w2_words, 0, 1)
        load_scales("w2", w2_s, w2_scales, 0, 2)
        load_saved("a1", a1_t, a1, 1, 2)
        load_words("w2", w2_w, w2_words, 1, 2)
        load_saved("a3", a3_t, a3, 0, 2)
        load_saved("a1", a1_t, a1, 2, 4)
        load_scales("w2", w2_s, w2_scales, 2, 4)
        load_words("w2", w2_w, w2_words, 2, 3)
        load_scales("w3", w3_s, w3_scales, 0, 4)
        load_words("w3", w3_w, w3_words, 0, 1)
        load_words("w1", w1_w, w1_words, 0, 1)
        load_scales("w1", w1_s, w1_scales, 0, 4)
        load_words("w2", w2_w, w2_words, 3, 4)
        load_saved("a3", a3_t, a3, 2, 4)
        load_words("w1", w1_w, w1_words, 1, 2)
        load_words("w3", w3_w, w3_words, 1, 2)
        load_words("w1", w1_w, w1_words, 2, 4)
        load_words("w3", w3_w, w3_words, 2, 4)

        g_w, g_s = {}, {}

        def gather_scales(lo, hi):
            picks = offsets[:, lo * LIST_COLS : hi * LIST_COLS]
            for s in range(PASSES):
                scales = v_tile([P, (hi - lo) * C], U8)
                nc.vector.tensor_copy(scales[:], dy_s[:, s, :].indirect(picks))
                for e in range(lo, hi):
                    g_s[e, s] = scales[:, (e - lo) * C : (e - lo + 1) * C]

        def gather_words(lo, hi):
            picks = offsets[:, lo * LIST_COLS : hi * LIST_COLS]
            for s in range(PASSES):
                words = v_tile([P, (hi - lo) * C], U32)
                nc.vector.tensor_copy(words[:], dy_w[:, s, :].bitcast(U32).indirect(picks))
                for e in range(lo, hi):
                    g_w[e, s] = words[:, (e - lo) * C : (e - lo + 1) * C]

        windows = [place("window_%d" % kt, [P, T], F32) for kt in range(KT)]
        silu_neg, a1_ps, tanh_half, gated_sig, factor1, rest = ({} for i in range(6))
        y_sb, y_ps, dh_ps, da, da_mx, dx_ps, dx_sb = ({} for i in range(7))

        def by_pairs(ap):
            return ap.rearrange("p t (c i) -> p c t i", i=2)

        def function(func, src, **affine):
            result = s_tile([P, 4, C], F32)[:]
            nc.scalar.activation(result, src, func, **affine)
            return result

        def turn(src):
            turned = bank([P, 4, P])
            for t in range(4):
                nc.tensor.transpose(turned[:, t, :], src[:, t, :], ident[:])
            return turned[:]

        def first_product(e):
            sums = bank([P, H])
            for s in range(PASSES):
                nc.tensor.matmul_mx(
                    sums[:], lhsT=g_w[e, s].bitcast(FP8X4), lhsT_scale=g_s[e, s],
                    rhs=w2_w[e][:, s, :].bitcast(FP4X4), rhs_scale=w2_s[e][:, s, :],
                    start=(s == 0), stop=(s == PASSES - 1),
                )
            dh_ps[e] = sums[:].rearrange("c (p t) -> c t p", t=4)

        def negative_silu(e):
            silu_neg[e] = function(ACT.Silu, a1_t[e], scale=-1.0)

        def gate_sigmoid(e):
            half = gate_half[:, e : e + 1]
            gated_sig[e] = function(ACT.Identity, tanh_half[e], scale=half, bias=half)

        def spread_gate():
            gate_ps = bank([P, P])
            nc.tensor.transpose(gate_ps[:], gate_rows[:], ident[:])
            half = s_tile([P, E], F32)
            nc.scalar.activation(half[:], gate_ps[:, 0:E], ACT.Copy, scale=0.5)
            return half

        def make_y(e):
            y_sb[e] = v_tile([P, 4, P], F32)[:]
            nc.vector.tensor_tensor(y_sb[e], dh_ps[e], gated_sig[e], ALU.mult)

        def make_rest(e, at=None, on_scalar=False):
            rest[e] = place("rest_%d" % e, [P, 4, C], F32, at)[:]
            if on_scalar:
                nc.scalar.activation(rest[e], silu_neg[e], ACT.Copy, scale=-1.0, bias=1.0)
            else:
                nc.gpsimd.tensor_scalar(rest[e], silu_neg[e], -1.0, 1.0, ALU.mult, ALU.add)

        def sigmoid_part(e):
            tanh_half[e] = function(ACT.Tanh, a1_ps[e], scale=0.5)

        def make_slope(e, at=None):
            factor1[e] = place("slope_%d" % e, [P, 4, C], F32, at)[:]
            nc.gpsimd.tensor_tensor(factor1[e], rest[e], a3_t[e], ALU.mult)

        def make_da(e, which, at=None):
            da[e, which] = v_tile([P, C, 4], BF16) if at is None else place("da_%d_%d" % (e, which), [P, C, 4], BF16, at)
            factor = (a1_t, factor1)[which][e]
            nc.vector.tensor_tensor(
                da[e, which][:].rearrange("p (c i) t -> p c t i", i=2), by_pairs(y_ps[e]), by_pairs(factor), ALU.mult
            )

        def quantize(e, which):
            codes = v_tile([P, C], U32)
            da_s = place("da_s_%d_%d" % (e, which), [P, C], U8)
            nc.vector.quantize_mx(codes[:].bitcast(FP8X4), da_s[:], da[e, which][:].rearrange("p j t -> p (j t)"))
            da_mx[e, which] = codes, da_s

        def second_product(e):
            dx_ps[e] = [bank([P, 2, C])[:] for h in range(2)]
            for kt in range(KT):
                for which, (words, plane) in enumerate(((w3_w, w3_s), (w1_w, w1_s))):
                    codes, da_s = da_mx[e, which]
                    nc.tensor.matmul_mx(
                        dx_ps[e][kt // 2][:, kt % 2, :],
                        lhsT=words[e][:, 0, kt * 256 : (kt + 1) * 256].bitcast(FP4X4),
                        lhsT_scale=plane[e][:, 0, kt * P : (kt + 1) * P],
                        rhs=codes[:].bitcast(FP8X4), rhs_scale=da_s[:],
                        start=(which == 0), stop=(which == 1),
                    )

        def copy_out(e, h, on_scalar):
            if on_scalar:
                dx_sb[e, h] = s_tile([P, 2, C], F32)[:]
                nc.scalar.copy(dx_sb[e, h], dx_ps[e][h])
            else:
                dx_sb[e, h] = v_tile([P, 2, C], F32)[:]
                nc.vector.tensor_copy(dx_sb[e, h], dx_ps[e][h])

        def scatter(e, kt, on_scalar):
            picks = offsets[:, e * LIST_COLS : (e + 1) * LIST_COLS]
            if on_scalar:
                nc.scalar.activation(windows[kt][:].indirect(picks), dx_sb[e, kt // 2][:, kt % 2, :], ACT.Copy)
            else:
                nc.vector.tensor_copy(windows[kt][:].indirect(picks), dx_sb[e, kt // 2][:, kt % 2, :])
            if e == E - 1:
                queue = nc.scalar if kt == LAST_WINDOW else nc.sync
                queue.dma_start(out=out[kt * P : (kt + 1) * P, :], in_=windows[kt][:])

        gather_scales(0, 2)
        gather_words(0, 1)
        gather_words(1, 2)
        gather_scales(2, 4)
        gather_words(2, 4)
        negative_silu(0)
        a1_ps[0] = turn(a1_t[0])
        gate_half = spread_gate()
        sigmoid_part(0)
        make_rest(0, on_scalar=True)
        gate_sigmoid(0)
        first_product(0)
        a1_ps[1] = turn(a1_t[1])
        make_y(0)
        negative_silu(1)
        sigmoid_part(1)
        first_product(1)
        y_ps[0] = turn(y_sb[0])
        gate_sigmoid(1)
        make_rest(1, 24 * KB)
        make_slope(0, 26 * KB)
        make_slope(1)
        make_y(1)
        a1_ps[2] = turn(a1_t[2])
        y_ps[1] = turn(y_sb[1])
        a1_ps[3] = turn(a1_t[3])
        sigmoid_part(2)
        negative_silu(2)
        gate_sigmoid(2)
        sigmoid_part(3)
        negative_silu(3)
        gate_sigmoid(3)
        make_da(0, 0)
        make_da(0, 1, 2 * KB)
        first_product(2)
        make_da(1, 0)
        quantize(0, 0)
        quantize(0, 1)
        second_product(0)
        make_da(1, 1, 12 * KB)
        make_rest(2, 1 * KB)
        make_rest(3, 24 * KB)
        make_y(2)
        first_product(3)
        y_ps[2] = turn(y_sb[2])
        quantize(1, 0)
        quantize(1, 1)
        copy_out(0, 0, True)
        copy_out(0, 1, True)
        scatter(0, 0, True)
        scatter(0, 1, True)
        scatter(0, 2, True)
        scatter(0, 3, True)
        make_y(3)
        y_ps[3] = turn(y_sb[3])
        second_product(1)
        make_slope(2, 11 * KB)
        make_slope(3, 1 * KB)
        make_da(2, 0)
        make_da(3, 0)
        make_da(2, 1)
        copy_out(1, 0, True)
        quantize(2, 0)
        quantize(2, 1)
        second_product(2)
        make_da(3, 1)
        copy_out(1, 1, False)
        scatter(1, 0, True)
        scatter(1, 1, True)
        quantize(3, 0)
        quantize(3, 1)
        second_product(3)
        scatter(1, 2, False)
        scatter(1, 3, False)
        copy_out(2, 0, True)
        copy_out(2, 1, True)
        scatter(2, 0, True)
        scatter(2, 1, True)
        copy_out(3, 0, False)
        copy_out(3, 1, False)
        scatter(2, 2, True)
        scatter(2, 3, True)
        scatter(3, 0, False)
        scatter(3, 1, False)
        scatter(3, 2, False)
        scatter(3, 3, True)
